import numpy as np, ml_dtypes
CORES = [24,25,26,27,28,29,30,31]
N = 8
import mx_ref
BF = ml_dtypes.bfloat16
def gcols(t, e):
    v = np.concatenate([t.reshape(8, 16, -1, 4), np.zeros((8, 16, 1, 4), BF)], axis=2)
    return np.ascontiguousarray(np.stack([v[g][:, e[g]] for g in range(8)])).reshape(128, -1)
def tile(rs):
    return np.stack(rs, axis=2).reshape(128, -1).astype(BF)
def cut(t, i, w=512):
    return t[:, w * i:w * i + w]
def pick(q, e):
    c = np.concatenate([q[0].reshape(128, -1, 4), np.zeros((128, 1, 4), np.uint8)], axis=1); s = np.concatenate([q[1], np.ones((16, 1), np.uint8)], axis=1)
    return (np.ascontiguousarray(c[:, e].reshape(128, -1)), np.ascontiguousarray(s[:, e]))
def join(*qs):
    return (np.concatenate([q[0] for q in qs], axis=1), np.concatenate([q[1] for q in qs], axis=1))
def put(q, e, v):
    c, s = q[0].reshape(128, -1, 4).copy(), q[1].copy(); c[:, e] = v[0].reshape(128, -1, 4); s[:, e] = v[1]
    return (c.reshape(128, -1), s)
def pk(c, s):
    return (np.ascontiguousarray(c), mx_ref.live(s))
def emit(q):
    return q[0], q[1]
def packed(v, rng):
    q = [mx_ref.quantize(np.ascontiguousarray(v[r])) for r in range(N)]
    return np.stack([a for a, b in q]), np.stack([mx_ref.plane(b, rng) for a, b in q])
def values_of_codes():
    e, c = np.zeros((128, 128, 4), np.float32), np.zeros((128, 2, 4), np.uint8)
    e[np.arange(128), np.arange(128), 0] = 1
    c[:127, :, 0] = np.arange(256).reshape(2, 128).T[:127]
    return mx_ref.matmul(mx_ref.quantize(e.reshape(128, 512).astype(BF)), (c.reshape(128, 8), np.full((16, 2), 127, np.uint8))).T.reshape(-1).astype(np.float64)
CODE_VALUE, SCALE_VALUE = values_of_codes(), 2.0 ** (np.arange(256) - 127.0)
def decode(q):
    return (CODE_VALUE[q[0]].reshape(16, 8, -1, 4) * SCALE_VALUE[q[1]][:, None, :, None] + 0.0).reshape(128, -1).astype(np.float32)
def f(rng, *shape):
    return mx_ref.flush((rng.standard_normal(shape, dtype=np.float32) * np.exp2(rng.integers(-2, 3, shape[:-1] + (1,)))).astype(BF))
def wide(rng, *shape, cols=0):
    v = rng.standard_normal(shape, dtype=np.float32) * np.exp2(rng.integers(-12, 13, shape)).astype(np.float32)
    if cols: v *= np.repeat(np.exp2(rng.integers(-cols, cols + 1, shape[:-2] + (1, shape[-1] // 4))) * (rng.random(shape[:-2] + (1, shape[-1] // 4)) > 0.0625), 4, axis=-1).astype(np.float32)
    return mx_ref.flush(v.astype(BF))
C, H, A, L, R = 256, 4, 8, 64, 3
def buckets(p):
    bit = p.reshape(8, 16, C)[:, :H] + np.float32(0.0) >= 0
    leaf = np.zeros((8, C), np.int64)
    for i in range(H): leaf = 2 * leaf + bit[:, i]
    at, slot = np.full((8, C), -1), np.zeros((8, C), np.int64)
    before = np.arange(C)[:, None] > np.arange(C)
    for v in range(H, -1, -1):
        way = (1 << v) - 1 + (leaf >> (H - v))
        free = at < 0
        n = np.sum((way[:, :, None] == way[:, None, :]) & free[:, None, :] & before, axis=2)
        new = free & (n < A)
        at[new] = way[new]
        slot[new] = n[new]
    return at, slot
def mates(at, slot):
    own = np.tile(np.arange(C), (8, 1))
    held = np.full((8, 2 << H, A), -1)
    g, j = np.nonzero(at >= 0)
    held[g, at[g, j], slot[g, j]] = j
    e = held[np.arange(8)[:, None], (at - 1) // 2, slot]
    return np.where((at > 0) & (e >= 0), e, own)
def big(v):
    v = v.astype(np.float32)
    v[np.abs(v) < np.float32(2.0 ** -16)] = 0
    return v.astype(BF)
def numbers_of(rng):
    return {"x": big(f(rng, N, 128, 4 * C)), "u": np.array(f(rng, N, 128, 512)), "v": np.array(f(rng, N, 128, 512))}
def weights(rng, w):
    c, p = packed(w, rng)
    return {"wc": c, "ws": p}
def still(rng, k, more=0):
    w = np.zeros((N, 128, 4, 128, 4), np.float32)
    i = np.arange(128)
    for b in range(4): w[:, i, b, i, b] = k
    e = i[15::16]
    w[:, e, 0, e, 1] = more
    return weights(rng, w.reshape(N, 128, 2048).astype(BF))
MARKS = np.array([[[0, 1], [1, 2], [0, 1], [1, 2], [1, 0], [1, 1], [2, 1], [0, 0]],
                  [[0, 1], [1, 2], [1, 1.125], [1.25, 1.375], [1, 0], [1, 1], [1.125, 1], [0, 0]]])
EDGES = [(12, 0), (12, 1), (11, 7)]
def marked(rng, d, leaf, size, k):
    x = d["x"].reshape(N, 8, 16, C, 4)
    u = d["u"].reshape(N, 128, 128, 4)
    x[:, :, :8] = 0
    fine = (size < 1).astype(int)[:, None, None]
    for i in range(H):
        bit = leaf >> (H - 1 - i) & 1
        x[:, :, i, :, :2] = (MARKS[fine, 4 * bit + rng.integers(0, 4, bit.shape)] * size[:, None, None, None]).astype(BF)
        for c in range(i, 128, 16):
            u[:, :, c] = 0
            u[:, c, c, 0] = k.astype(BF)
            u[:, c, c, 1] = (-k).astype(BF)
    return {"x": x.reshape(N, 128, 4 * C), "u": u.reshape(N, 128, 512), "v": d["v"]}
def setup_inputs(rng):
    return {**numbers_of(rng), **weights(rng, big(f(rng, N, 128, 2048)))}
def setup_inputs_leaves(rng):
    d = numbers_of(rng)
    o = rng.permutation(N)
    leaf = rng.integers(0, 1 << H, (N, 8, C))
    s = np.repeat(np.arange(8), [A, A, A + A // 2, 2 * A - A // 2, A + 1, 0, 0, A - 1])
    for r in range(N):
        for g in range(8):
            m = int(rng.integers(1 << H))
            if o[r] == 0: leaf[r, g] = m
            if o[r] == 1: leaf[r, g] = rng.permutation(np.concatenate([s, rng.integers(8, 1 << H, C - len(s))])) ^ m
            if o[r] == 3 and g % 4 == 0: leaf[r, g] = rng.permutation(np.arange(C) % (1 << H))
            if o[r] == 3 and g % 4 > 0:
                n, p = EDGES[g % 4 - 1]
                leaf[r, g] = rng.permutation(np.concatenate([n - 1 - np.arange(C - p) % n, np.full(p, n)])) ^ m
    d = marked(rng, d, leaf, np.ones(N), np.ones(N, np.float32))
    d["x"][o == 2] = 0
    return {**d, **still(rng, 64)}
def setup_inputs_near(rng):
    o = rng.permutation(N) % 4
    size = 2.0 ** np.array([-30.0, -30.0, 0.0, 10.0])[o]
    k = np.where(o < 2, 2.0 ** -30, 1.0).astype(np.float32)
    leaf = rng.integers(0, 1 << H, (N, 8, C)) & rng.integers(0, 1 << H, (N, 8, 1))
    return {**marked(rng, numbers_of(rng), leaf, size, k), **still(rng, 64)}
def setup_inputs_again(rng):
    d = numbers_of(rng)
    u = d["u"].reshape(N, 128, 128, 4)
    for g in range(0, 128, 16):
        for c in range(g, g + H):
            u[:, :, c] = 0
            u[:, c, c, 0] = 1
            u[:, c + 8, c, 0] = -1
    s = (N, 8, 16, C, 4)
    x = rng.integers(8, 16, s) * np.exp2(rng.integers(-21, -12, s))
    x[:, :, 8:8 + H, :, 0] = x[:, :, :H, :, 0] * rng.integers(1, 3, (N, 8, H, C))
    x[:, :, 7, :, 0] = 1.9921875
    x[:, :, 15, :, 0] = 1.875
    x[:, :, 15, :, 1] = 0.75
    return {"x": x.astype(np.float32).astype(BF).reshape(N, 128, 4 * C), "u": u.reshape(N, 128, 512), "v": d["v"], **still(rng, 64, 8)}
def setup_inputs_huge(rng):
    d = numbers_of(rng)
    o = rng.permutation(N)
    c = np.ones((N, C))
    s = rng.choice([-1.0, 1.0], (N, 128))
    for r in range(N):
        if o[r] == 0: s[r] = -1
        if o[r] == 1: s[r] = 1
        if o[r] > 2: c[r] = rng.permutation(C) % 2 * 2.0 - 1.0
    x = 2.0 ** 28 * (1.5 + 0.5 * rng.random((N, 128, C, 4))) * c[:, None, :, None]
    u = 2.0 ** 30 * (0.75 + 0.25 * rng.random((N, 128, 128, 4))) * s[:, None, :, None]
    return {"x": x.astype(np.float32).astype(BF).reshape(N, 128, 4 * C), "u": u.astype(np.float32).astype(BF).reshape(N, 128, 512), "v": d["v"], **still(rng, 32)}
def setup_inputs_spread(rng):
    d = setup_inputs(rng)
    d["x"] = big(wide(rng, N, 128, 4 * C, cols=6))
    return d
def check_inputs(d):
    b = []
    for k in ("x", "u", "v"):
        a = np.abs(d[k].astype(np.float32))
        if not (np.isfinite(a).all() and ((a == 0) | (a >= 2.0 ** -30) & (a <= 2.0 ** 30)).all()): b.append("a value of " + k)
    return b
def reference(x, u, v, wc, ws):
    qu = [mx_ref.quantize(u[r]) for r in range(N)]
    lay = [pk(wc[r], ws[r]) for r in range(N)]
    now = [x[r] for r in range(N)]
    for t in range(R):
        held, made, gone, sent = [], [], [], []
        for r in range(N):
            at, slot = buckets(mx_ref.matmul(qu[r], mx_ref.quantize(now[r])))
            met = gcols(now[r], mates(at, slot))
            q = mx_ref.quantize((now[r].astype(np.float32) + met.astype(np.float32)).astype(BF))
            h = tile([mx_ref.matmul(pick(lay[r], np.arange(128 * b, 128 * b + 128)), q) * np.float32(0.015625) for b in range(4)])
            e = np.argsort(at, axis=1, kind="stable")[:, :L]
            held.append(at)
            made.append(h)
            gone.append(e)
            sent.append(mx_ref.quantize(gcols(h, e)))
        came = decode(join(*sent)).astype(BF)
        for r in range(N):
            e = np.tile(np.arange(C), (8, 1))
            np.put_along_axis(e, gone[r], np.tile(C + np.arange(L), (8, 1)), axis=1)
            now[r] = gcols(np.concatenate([made[r], cut(came, (r - 1) % N, 4 * L)], axis=1), e)
    y, ob = np.zeros((N, 128, C), np.float32), np.zeros((N, 8, C), np.float32)
    oc, osc = np.zeros((N, 128, 4 * C), np.uint8), np.zeros((N, 16, C), np.uint8)
    for r in range(N):
        q = mx_ref.quantize(now[r])
        y[r] = mx_ref.matmul(mx_ref.quantize(v[r]), q)
        ob[r] = held[r]
        oc[r], osc[r] = emit(q)
    return {"y": y, "ob": ob, "oc": oc, "osc": osc}

@@ -1,0 +1,397 @@
+import numpy as np
+from concourse.bass import DstId, RemoteDMATransfer
+from concourse.mybir import dt, AluOpType, AxisListType, ActivationFunctionType
+
+A = AluOpType
+F = ActivationFunctionType
+ROUNDS = 3
+BIG = 1024.0
+SCRATCH = {}
+for _d, _l in {
+    "bfloat16": dict(us=512, vs=512, kt=1040, kin=[2, 144], et=516, ones=516, zero=260, zero2=512, st=512, bt=512, zt=1024, came=256, junk=256,
+                     dd=[2, 512], mz=288, s4=256, x0=1024, x1=1024, x2=1024, x3=1024, xw0=2048, xw1=2048, xw2=2048),
+    "float8_e4m3fn_x4": dict(qu=128, qv=128, qw=512, qx=256, qz=256, qs=128, qk=512, qe=512, ql0=320, ql1=320, ql2=320),
+    "uint8": dict(su=128, sv=128, sw=512, sx=256, sz=256, ss=128, sk=512, se=512, sl0=512, sl1=512, sl2=512),
+    "float16": dict(ab=[4, 146], cs=[2, 144], d4=[9, 2, 16], w=576, in3=288, in2=144, in1=36, in0=18, pen=512, wk=512, sp=512, sm=512,
+                    mm=256, mx4=256),
+    "float32": dict(ksrc=[2, 4], fb=26, car=2, cd=[2, 33], m8=64, k8=64, mk=64, me=64, me8=64, val=256, val0=256, own=256, own0=256, own1=256,
+                    dl=8, da=8, th=8, dj=16, kc=32, kc0=32, cmp=32, prod=32, s8=32, i4=4, att=512, atr=256, ys=256, tab0=512, tab1=512, tab2=512),
+    "int32": dict(pi=2, ib=10),
+    "uint16": dict(opos=16, omp=16, oz=64, oi=4, oe=16, onat=16, lt=2, lj=2),
+}.items():
+    for _n, _s in _l.items():
+        SCRATCH[_n] = ("sbuf", [128] + (_s if isinstance(_s, list) else [_s]), _d)
+for _t in range(8):
+    SCRATCH["ps%d" % _t] = ("psum", [128, 512], "float32")
+
+SEMAPHORES = ["v", "a", "p", "g", "ldx", "ldy", "ldu", "ldw", "lds", "ldv", "ld0", "sent0", "sent1", "sent2", "arr0", "arr1", "arr2", "out"]
+
+
+def rank_program(g, core, T, topo):
+    rank = T.rank_of(core)
+    if rank is None:
+        return
+    nxt = T.cores[(rank + 1) % len(T.cores)]
+    rid, pid, _ = topo.addr(nxt)
+    eng = topo.engines(core, nxt)
+
+    Q = {"v": g.vector, "a": g.scalar, "p": g.tensor, "g": g, "s": g.sync}
+    V = g.vector
+    count = {}
+    known = {e: {} for e in Q}
+    log = {}
+    s = slice
+
+    def N(name, *idx):
+        where, shape, _d = SCRATCH[name]
+        m = np.zeros(shape, bool)
+        m[s(None) if where == "psum" else idx] = True
+        return (T[name][idx if len(idx) > 1 else idx[0]], name, m, where == "psum")
+
+    def R(name, a=None, b=None, c=None):
+        return N(name, s(None)) if a is None else N(name, s(None), s(a, b, c))
+
+    def R3(name, *idx):
+        return N(name, s(None), *idx)
+
+    def col(name, c):
+        return R(name, c, c + 1)
+
+    def wait(e, tok):
+        sem, val, clock = tok
+        if known[e].get(sem, 0) >= val:
+            return
+        Q[e].wait_ge(T.sem[sem], val)
+        known[e][sem] = val
+        for k2, v2 in clock.items():
+            known[e][k2] = max(known[e].get(k2, 0), v2)
+
+    def order(e, reads, writes):
+        deps = {}
+        for r, wr in [(x, x[3]) for x in reads] + [(x, True) for x in writes]:
+            for m, tok, w2 in log.get(r[1], []):
+                if (wr or w2) and known[e].get(tok[0], 0) < tok[1] and deps.get(tok[0], (0, 0))[1] < tok[1] and (m & r[2]).any():
+                    deps[tok[0]] = tok
+        for tok in sorted(deps.values(), key=lambda t: -len(t[2])):
+            wait(e, tok)
+
+    def note(tok, reads, writes):
+        for r in reads:
+            log.setdefault(r[1], []).append((r[2], tok, r[3]))
+        for r in writes:
+            log.setdefault(r[1], []).append((r[2], tok, True))
+
+    def op(e, make, reads, writes, sem=None, inc=1):
+        reads = [x for x in reads if isinstance(x, tuple)]
+        order(e, reads, writes)
+        sem = sem or e
+        make().then_inc(T.sem[sem], inc)
+        count[sem] = count.get(sem, 0) + inc
+        tok = (sem, count[sem], dict(known[e]))
+        note(tok, reads, writes)
+        return tok
+
+    def ap(x, off=None):
+        if off:
+            return x[0].indirect(off[0])
+        return x[0] if isinstance(x, tuple) else x
+
+    def ts(out, in0, s1, s2, *o):
+        op("v", lambda: V.tensor_scalar(out[0], in0[0], ap(s1), ap(s2), *o), [in0, s1, s2], [out])
+
+    def tt(out, in0, in1, o, off=None):
+        op("v", lambda: V.tensor_tensor(out[0], ap(in0, off), in1[0], o), [in0, in1, off], [out])
+
+    def cp(out, in_, off=None):
+        op("v", lambda: V.tensor_copy(out[0], ap(in_, off)), [in_, off], [out])
+
+    def scatter(win, off, in_):
+        op("v", lambda: V.tensor_copy(ap(win, off), in_[0]), [in_, off], [win])
+
+    def scan(out, d0, d1, init, o0, o1):
+        op("v", lambda: V.tensor_tensor_scan(out[0], d0[0], d1[0], ap(init), o0, o1), [d0, d1, init], [out])
+
+    def tr(out, in_):
+        op("v", lambda: V.transpose(out[0], in_[0]), [in_], [out])
+
+    def fill(out, c):
+        op("v", lambda: V.memset(out[0], c), [], [out])
+
+    def quant(n, a, in_):
+        q, sc = R("q" + n, a, a + 128), R("s" + n, a, a + 128)
+        op("v", lambda: V.quantize_mx(q[0], sc[0], in_[0]), [in_], [q, sc])
+
+    def PS(bank, a=0):
+        return R("ps%d" % bank, a, 128)
+
+    def mm(bank, w, wa, x, xa):
+        o, a, b, c, d = PS(bank), R("q" + w, wa, wa + 128), R("s" + w, wa, wa + 128), R("q" + x, xa, xa + 128), R("s" + x, xa, xa + 128)
+        op("p", lambda: g.tensor.matmul_mx(o[0], a[0], b[0], c[0], d[0], True, True), [a, b, c, d], [o])
+
+    def act(out, in_, fn=F.Copy, bias=None, scale=1.0, acc=None, off=None):
+        kw = {"scale": ap(scale)}
+        if bias is not None:
+            kw["bias"] = ap(bias)
+        if acc:
+            kw["accum_out"] = acc[0]
+        op("a", lambda: g.scalar.activation(out[0], ap(in_, off), fn, **kw), [in_, bias, scale, off], [out] + ([acc] if acc else []))
+
+    def iota(out, pat, base):
+        op("g", lambda: g.iota(out[0], pat, base, 0, allow_small_or_imprecise_dtypes=True), [], [out])
+
+    def u8(x):
+        return x[0].bitcast(dt.uint8) if x[1][0] == "q" else x[0]
+
+    def load(e, dst, src, sem):
+        return op(e, lambda: Q[e].dma_start(u8(dst), src), [], [dst], sem=sem, inc=16)
+
+    def store(e, dst, src):
+        order(e, [src], [])
+        Q[e].dma_start(dst, u8(src)).then_inc(T.sem.out, 16)
+        count["out"] = count.get("out", 0) + 16
+
+    load("a", R("us"), T.u[:], "ldu")
+    load("s", R("x0", 0, 512), T.x[:, 0:512], "ldx")
+    wait("s", load("s", R("x0", 512, 1024), T.x[:, 512:1024], "ldy"))
+    load("s", R("qw"), T.wc[:], "ldw")
+    load("s", R("sw"), T.ws[:], "lds")
+    load("s", R("xw0", 0, 1024), T.x[:], "ld0")
+    load("s", R("vs"), T.v[:], "ldv")
+
+    op("g", lambda: g.iota(T.pi[:, 0:1], [[0, 1]], 0, 1), [], [col("pi", 0)])
+    for k, (pats, bases) in enumerate([([[[8, 16]], [[8, 8]], [[8, 4]], [[8, 2]]], [120, 56, 24, 8]),
+                                       ([[[8, 8], [0, 2]], [[8, 4], [0, 2]], [[8, 2], [0, 2]], [[0, 2]]], [56, 24, 8, 0])]):
+        for lv in range(4):
+            iota(R3("cd", k, s(1 << lv, 33 if lv else 32, 2 << lv)), pats[lv], bases[lv])
+    iota(R3("cd", s(0, 2), s(0, 33, 32)), [[0, 2], [2336, 2]], -2000)
+    iota(R3("cd", s(0, 2), s(16, 17)), [[-16, 2]], 0)
+    iota(R("i4"), [[1, 4]], 0)
+    iota(R("val0"), [[64, 8], [512, 2], [4, 16]], -1024)
+    iota(R("own0"), [[4, 256]], 4096)
+    iota(R("kc0"), [[16, 4], [0, 8]], 0)
+    iota(R("mz"), [[0, 144], [1, 2]], 0)
+    iota(R("dl", 0, 3), [[4, 3]], 0)
+    iota(R("da", 2, 8), [[0, 6]], 8)
+    iota(col("da", 1), [[0, 1]], 256)
+    iota(R("dj"), [[0, 4], [16, 4]], 0)
+    iota(R("tab0"), [[0, 512]], 4096)
+    iota(R("s4"), [[0, 256]], 0)
+    iota(R("m8"), [[0, 64]], 1)
+    iota(R("k8"), [[0, 8], [1, 8]], 0)
+    iota(R("s4", 0, 256, 4), [[0, 64]], -8192)
+    iota(R("m8", 0, 64, 8), [[0, 8]], 0)
+    iota(R("bt", 256, 512), [[0, 256]], 0)
+    iota(R("zero2"), [[0, 512]], 0)
+    iota(R("ones"), [[0, 516]], 1)
+    op("g", lambda: g.affine_select(T.et[:], T.ones[:], [[-1, 516]], A.is_equal, 0.0, 3, 4), [R("ones")], [R("et")])
+
+    fill(R("zero"), 0.0)
+    act(R("kt", 2, 1040, 4), R("zero"))
+    act(R("kt", 3, 1040, 4), R("zero"))
+    act(R("kt", 512, 1040, 520), R("zero", 0, 2))
+    act(R("st", 2, 512, 4), R("zero", 0, 128))
+    act(R("st", 3, 512, 4), R("zero", 0, 128))
+    for c, sh in enumerate([3, 2, 1, 0, 4]):
+        ts(col("ib", c), col("pi", 0), sh, 1, A.logical_shift_right, A.bitwise_and)
+    fill(R("kin"), 0.0)
+    cp(R("fb", 0, 5), R("ib", 0, 5))
+    ts(col("ib", 5), col("pi", 0), 3, None, A.bitwise_and)
+    ts(R("fb", 12, 16), R("fb", 0, 4), 2.0, -1.0, A.mult, A.add)
+    ts(col("fb", 16), col("fb", 4), -1.0, 1.0, A.mult, A.add)
+    ts(col("ib", 6), col("pi", 0), 2, 3, A.logical_shift_right, A.bitwise_and)
+    ts(R3("ksrc", 1, s(0, 4)), R("fb", 12, 16), col("fb", 4), None, A.mult)
+    ts(R3("ksrc", 0, s(0, 4)), R("fb", 12, 16), col("fb", 16), None, A.mult)
+    op("v", lambda: V.tensor_reduce(T.fb[:, 17:18], T.fb[:, 0:4], AxisListType.X, A.add), [R("fb", 0, 4)], [col("fb", 17)])
+    for a in range(4):
+        cp(N("kin", s(32 * a, 32 * a + 32), s(0, 2), s(16 + 32 * a, 20 + 32 * a)), N("ksrc", s(32 * a, 32 * a + 32), s(0, 2), s(0, 4)))
+    ts(col("ib", 7), col("pi", 0), 15, None, A.bitwise_and)
+    for y in range(2):
+        for var in range(2):
+            tr(R("kt", 520 * y + var, 520 * y + 512, 4), R3("kin", var, s(16 - 16 * y, 144 - 16 * y)))
+    ts(col("ib", 8), col("pi", 0), 7, None, A.bitwise_and)
+    for y in range(2):
+        quant("k", 128 * y, R("kt", 520 * y, 520 * y + 512))
+    quant("u", 0, R("us"))
+
+    def constants_1():
+        ts(col("fb", 18), col("fb", 16), -10.0, 1.0, A.mult, A.add)
+        cp(R("fb", 5, 9), R("ib", 5, 9))
+        tt(col("fb", 19), col("fb", 18), col("fb", 17), A.subtract)
+        cp(R3("ab", s(0, 4), s(129, 145)), R("zero", 0, 64))
+        cp(R3("ab", s(0, 4), s(0, 1)), R("zero", 0, 4))
+
+    def ramps():
+        tt(R3("dd", s(0, 2), s(0, 32)), R3("cd", s(0, 2), s(0, 32)), R3("cd", s(0, 2), s(1, 33)), A.subtract)
+        for n in (32, 64, 128, 256):
+            act(R3("dd", s(0, 2), s(n, 2 * n)), R3("dd", s(0, 2), s(0, n)))
+
+    def masks():
+        ts(R("fb", 20, 24), R("i4"), col("fb", 6), None, A.is_equal)
+        act(R("val"), R("val0"), F.Identity, bias=col("fb", 5))
+        act(R("kc"), R("kc0"), F.Identity, bias=col("fb", 7))
+        act(R("own1"), R("own0"), F.Identity, bias=col("fb", 5))
+        for k in range(4):
+            act(R("own", k, 256, 4), R("own1", k, 256, 4), F.Identity, bias=-4096.0, scale=col("fb", 20 + k))
+
+    small = [
+        ramps,
+        masks,
+        lambda: ts(col("fb", 9), col("fb", 8), 0.0, None, A.is_equal),
+        lambda: ts(R("lt"), R("i4", 0, 2), 0.0, col("fb", 8), A.mult, A.add),
+        lambda: ts(R("fb", 10, 12), R("i4", 0, 4, 2), col("fb", 0), 8.0, A.add, A.add),
+        lambda: ts(col("ib", 9), col("pi", 0), 1, 7, A.logical_shift_right, A.bitwise_and),
+        lambda: ts(R("lj"), R("fb", 10, 12), col("fb", 9), col("fb", 8), A.mult, A.add),
+        lambda: cp(col("fb", 24), col("ib", 9)),
+        lambda: ts(R("mk"), R("k8"), col("fb", 24), None, A.is_equal),
+        lambda: ts(col("fb", 25), col("fb", 3), 2.0, col("fb", 5), A.mult, A.subtract),
+    ]
+
+    def gap():
+        if small:
+            small.pop(0)()
+
+    def pen(a, c):
+        ts(R("pen", a, 512, c), R("w", a, 512, c), BIG, -BIG, A.is_gt, A.mult)
+
+    def knock(a, c):
+        scan(R("wk", a, 512, c), R("pen", a, 512, c), R("w", a, 512, c), 0.0, A.min, A.add)
+
+    for t in range(ROUNDS):
+        xn, xo, xw, tab, ln = "x%d" % (t + 1), "x%d" % t, "xw%d" % t, "tab%d" % t, "l%d" % t
+        for h in range(2):
+            quant("x", 128 * h, R(xo, 512 * h, 512 * h + 512))
+            mm(h, "u", 0, "x", 128 * h)
+        for h in range(2):
+            if t == 0:
+                quant("k", 256 + 128 * h, R("kt", 520 * h + 1, 520 * h + 513))
+            ts(R("st", h, 512, 4), PS(h), 0.0, None, A.is_ge)
+        quant("s", 0, R("st"))
+        if t == 0:
+            constants_1()
+        for y in range(2):
+            mm(2 + y, "k", 128 * y, "s", 0)
+            mm(4 + y, "k", 256 + 128 * y, "s", 0)
+            act(R("junk", 128 * y, 128 * y + 128), PS(4 + y), F.Relu, bias=col("fb", 19), acc=col("car", y))
+        if t > 0:
+            act(R(xw, 0, 1024), R(xo))
+            act(R(xw, 1024, 2048), R(xo))
+        for y in range(2):
+            ts(R3("ab", y, s(1, 129)), PS(2 + y), col("fb", 17), -BIG, A.is_equal, A.mult)
+        for y in range(2):
+            ts(R3("ab", 2 + y, s(1, 129)), R3("ab", y, s(1, 129)), -(1.0 + 1.0 / BIG), None, A.mult)
+        for y in range(2):
+            scan(R3("cs", y, s(0, 144)), R3("ab", y, s(0, 144)), R3("ab", 2 + y, s(1, 145)), col("car", y), A.add, A.add)
+        for y in range(2):
+            ts(R3("d4", s(0, 9), y, s(0, 16)), R3("cs", y, s(0, 144)), -8.0, 0.0, A.add, A.max)
+        gap()
+        tr(R("w", 0, 576, 2), R("d4"))
+        gap()
+        if t == 0:
+            act(R(xw, 1024, 2048), R(xo))
+        scan(R("in3"), R("mz"), R("w", 0, 576, 2), 0.0, A.mult, A.add)
+        gap()
+        pen(0, 2)
+        ts(R("w", 1, 576, 4), R("in3", 1, 288, 2), -8.0, 0.0, A.add, A.max)
+        gap()
+        knock(0, 2)
+        scan(R("in2"), R("mz", 0, 144), R("w", 1, 576, 4), 0.0, A.mult, A.add)
+        gap()
+        pen(1, 4)
+        ts(R("w", 3, 576, 8), R("in2", 1, 144, 2), -8.0, 0.0, A.add, A.max)
+        ts(R("dl", 5, 8), R("in2", 137, 142, 2), 8.0, None, A.min)
+        tt(R("in1"), R("w", 3, 576, 16), R("w", 11, 576, 16), A.add)
+        gap()
+        knock(1, 4)
+        ts(R("w", 7, 576, 16), R("in1"), -8.0, 0.0, A.add, A.max)
+        ts(R("dl", 3, 5), R("in1", 34, 36), 8.0, None, A.min)
+        tt(R("in0"), R("w", 7, 576, 32), R("w", 23, 576, 32), A.add)
+        gap()
+        ts(R("w", 15, 512, 32), R("in0", 0, 16), -8.0, None, A.add)
+        ts(R("w", 31, 512, 32), R("in0", 0, 16), -608.0, None, A.add)
+        ts(col("dl", 1), col("in0", 17), -8.0, None, A.add)
+        pen(3, 4)
+        scan(R("th"), R("dl"), R("dl"), 0.0, A.add, A.max)
+        knock(3, 4)
+        tt(R("dj", 1, 8), R("da", 1, 8), R("dl", 1, 8), A.subtract)
+        scan(R("sp"), R3("dd", 0, s(0, 512)), R("wk"), 0.0, A.add, A.max)
+        scan(R("sm"), R3("dd", 1, s(0, 512)), R("wk"), 0.0, A.add, A.max)
+        ts(R("opos"), R("sp", 31, 512, 32), -425.0, None, A.add)
+        for h in range(2):
+            ts(R("omp", 8 * h, 8 * h + 8), R("sm", 31 + 32 * h, 512, 64), -425.0, 248.0, A.add, A.max)
+        scatter(R(tab), R("opos"), R("val"))
+        tt(R("cmp"), R("th"), R("kc"), A.is_le, off=R("lt"))
+        tt(R("mm"), R(tab), R("own"), A.min, off=R("omp"))
+        tt(R("prod"), R("dj"), R("cmp"), A.mult, off=R("lj"))
+        scan(R("mx4"), R("s4"), R("mm"), 0.0, A.add, A.max)
+        scan(R("s8"), R("m8", 0, 32), R("prod"), 0.0, A.mult, A.add)
+        ts(R("oz"), R("mx4", 3, 256, 4), 1024.0, None, A.add)
+        ts(R("oi"), R("s8", 7, 32, 8), col("fb", 7), None, A.add)
+        gap()
+        gap()
+        for h in range(2):
+            tt(R("zt", 512 * h, 512 * h + 512), R(xw), R(xo, 512 * h, 512 * h + 512), A.add, off=R("oz", 32 * h, 32 * h + 32))
+            if h == 0:
+                tt(R("me"), R(tab), R("mk"), A.mult, off=R("oi"))
+            else:
+                scan(R("me8"), R("m8"), R("me"), 0.0, A.mult, A.add)
+            quant("z", 128 * h, R("zt", 512 * h, 512 * h + 512))
+            for b in range(4):
+                mm(4 * h + b, "w", 128 * b, "z", 128 * h)
+            if h == 0:
+                for b in range(4):
+                    act(R(xn, b, 512, 4), PS(b), scale=0.015625)
+        gap()
+        if t == 0:
+            quant(ln, 128, R("zero2"))
+        for k in range(2):
+            ts(R("oe", 8 * k, 8 * k + 8), R("me8", 7, 64, 8), col("fb", 25), 1024.0 + k, A.add, A.add)
+        for b in range(4):
+            if b % 2 == 0:
+                act(R(xn, 512 + b, 1024, 4), PS(4 + b), scale=0.015625)
+            else:
+                ts(R(xn, 512 + b, 1024, 4), PS(4 + b), 0.015625, None, A.mult)
+        act(R("bt", 1, 256, 2), R(xn), off=R("oe", 8, 16))
+        cp(R("bt", 0, 256, 2), R(xn), off=R("oe", 0, 8))
+        quant(ln, 0, R("bt"))
+        srcs = [R("q" + ln, 0, 64), R("s" + ln, 0, 256)]
+        dsts = [R("q" + ln, 256, 320), R("s" + ln, 256, 512)]
+        order("g", srcs, [])
+        per = len(eng) // 2
+        g.remote_dma_fused([RemoteDMATransfer(dst_ids=[DstId(rid=rid, pnc=pid)], dma_engine_mask=sum(1 << e for e in eng[per * k:per * k + per]),
+                                              remote_sem=T.sem["arr%d" % t], src=u8(srcs[k]), dst=u8(dsts[k])) for k in range(2)],
+                           local_sem=T.sem["sent%d" % t])
+        count["sent%d" % t] = count["arr%d" % t] = 2 * per
+        note(("arr%d" % t, 2 * per, {}), [], dsts)
+        if t == 0:
+            iota(R("tab1"), [[0, 512]], 4096)
+            iota(R("tab2"), [[0, 512]], 4096)
+            for b in (0, 2, 1, 3):
+                quant("e", 128 * b, R("et", 3 - b, 515 - b))
+        if t == 1:
+            iota(R("att", 0, 256), [[0, 256]], -1)
+            iota(R("att", 256, 512), [[1, 32], [0, 8]], 0)
+            quant("v", 0, R("vs"))
+        if t < ROUNDS - 1:
+            quant("l%d" % (t + 1), 128, R("zero2"))
+        else:
+            for h in range(2):
+                ts(R("onat", 8 * h, 8 * h + 8), R("sp", 31 + 32 * h, 512, 64), -425.0, None, A.add)
+            act(R("atr"), R("att"), off=R("onat"))
+            store("s", T.ob[:], N("atr", s(0, 128, 16), s(0, 256)))
+        for b in (0, 2, 1, 3):
+            mm(b, "e", 128 * b, ln, 192)
+            (act if b % 2 else cp)(R("came", 128 * (b % 2) + b // 2, 128 * (b % 2) + 128, 2), PS(b, 64))
+        for k in range(2):
+            scatter(R(xn), R("oe", 8 * k, 8 * k + 8), R("came", 128 * k, 128 * k + 128))
+
+    for h in range(2):
+        quant("x", 128 * h, R("x%d" % ROUNDS, 512 * h, 512 * h + 512))
+        mm(h, "v", 0, "x", 128 * h)
+    store("s", T.oc[:], R("qx"))
+    for k in range(4):
+        store("a", T.osc[4 * k:4 * k + 4, :], N("sx", s(32 * k, 32 * k + 4), s(0, 256)))
+    for h in range(2):
+        cp(R("ys", 128 * h, 128 * h + 128), PS(h))
+    store("s", T.y[:], R("ys"))
+    for sem, val in count.items():
+        wait("g" if sem in ("g", "sent0", "sent1", "sent2") else "s", (sem, val, {}))

@@ -12,7 +12,7 @@ for _d, _l in {
                      dd=[2, 512], mz=288, s4=256, x0=1024, x1=1024, x2=1024, x3=1024, xw0=2048, xw1=2048, xw2=2048),
     "float8_e4m3fn_x4": dict(qu=128, qv=128, qw=512, qx=256, qz=256, qs=128, qk=512, qe=512, ql0=320, ql1=320, ql2=320),
     "uint8": dict(su=128, sv=128, sw=512, sx=256, sz=256, ss=128, sk=512, se=512, sl0=512, sl1=512, sl2=512),
-    "float16": dict(ab=[4, 146], cs=[2, 144], d4=[9, 2, 16], w=576, in3=288, in2=144, in1=36, in0=18, pen=512, wk=512, sp=512, sm=512,
+    "float16": dict(ab=[4, 146], cs=[2, 144], d4=[9, 2, 16], w=576, in3=288, in2=144, in1=36, pen=512, wk=576, sp=512, sm=512,
                     mm=256, mx4=256),
     "float32": dict(ksrc=[2, 4], fb=26, car=2, cd=[2, 33], m8=64, k8=64, mk=64, me=64, me8=64, val=256, val0=256, own=256, own0=256, own1=256,
                     dl=8, da=8, th=8, dj=16, kc=32, kc0=32, cmp=32, prod=32, s8=32, i4=4, att=512, atr=256, ys=256, tab0=512, tab1=512, tab2=512),
@@ -68,16 +68,16 @@ def rank_program(g, core, T, topo):
 
     def order(e, reads, writes):
         deps = {}
-        for r, wr in [(x, x[3]) for x in reads] + [(x, True) for x in writes]:
+        for r, wr in [(x, False) for x in reads] + [(x, True) for x in writes]:
             for m, tok, w2 in log.get(r[1], []):
-                if (wr or w2) and known[e].get(tok[0], 0) < tok[1] and deps.get(tok[0], (0, 0))[1] < tok[1] and (m & r[2]).any():
+                if (wr or w2 or (r[3] and tok[0] != e)) and known[e].get(tok[0], 0) < tok[1] and deps.get(tok[0], (0, 0))[1] < tok[1] and (m & r[2]).any():
                     deps[tok[0]] = tok
         for tok in sorted(deps.values(), key=lambda t: -len(t[2])):
             wait(e, tok)
 
     def note(tok, reads, writes):
         for r in reads:
-            log.setdefault(r[1], []).append((r[2], tok, r[3]))
+            log.setdefault(r[1], []).append((r[2], tok, False))
         for r in writes:
             log.setdefault(r[1], []).append((r[2], tok, True))
 
@@ -159,21 +159,21 @@ def rank_program(g, core, T, topo):
     load("s", R("vs"), T.v[:], "ldv")
 
     op("g", lambda: g.iota(T.pi[:, 0:1], [[0, 1]], 0, 1), [], [col("pi", 0)])
-    for k, (pats, bases) in enumerate([([[[8, 16]], [[8, 8]], [[8, 4]], [[8, 2]]], [120, 56, 24, 8]),
-                                       ([[[8, 8], [0, 2]], [[8, 4], [0, 2]], [[8, 2], [0, 2]], [[0, 2]]], [56, 24, 8, 0])]):
+    for k, (pats, bases) in enumerate([([[[8, 16]], [[8, 8]], [[8, 4]], [[8, 2]]], [383, 319, 287, 271]),
+                                       ([[[8, 8], [0, 2]], [[8, 4], [0, 2]], [[8, 2], [0, 2]], [[0, 2]]], [319, 287, 271, 15])]):
         for lv in range(4):
             iota(R3("cd", k, s(1 << lv, 33 if lv else 32, 2 << lv)), pats[lv], bases[lv])
-    iota(R3("cd", s(0, 2), s(0, 33, 32)), [[0, 2], [2336, 2]], -2000)
-    iota(R3("cd", s(0, 2), s(16, 17)), [[-16, 2]], 0)
+    iota(R3("cd", s(0, 2), s(0, 33, 32)), [[0, 2], [2007, 2]], -2000)
+    iota(R3("cd", s(0, 2), s(16, 17)), [[-304, 2]], 7)
     iota(R("i4"), [[1, 4]], 0)
     iota(R("val0"), [[64, 8], [512, 2], [4, 16]], -1024)
     iota(R("own0"), [[4, 256]], 4096)
     iota(R("kc0"), [[16, 4], [0, 8]], 0)
     iota(R("mz"), [[0, 144], [1, 2]], 0)
     iota(R("dl", 0, 3), [[4, 3]], 0)
-    iota(R("da", 2, 8), [[0, 6]], 8)
-    iota(col("da", 1), [[0, 1]], 256)
-    iota(R("dj"), [[0, 4], [16, 4]], 0)
+    iota(R("da", 3, 8), [[0, 5]], 8)
+    iota(R("da", 1, 3), [[264, 2]], -8)
+    iota(R("dj"), [[0, 4], [16, 4]], 16)
     iota(R("tab0"), [[0, 512]], 4096)
     iota(R("s4"), [[0, 256]], 0)
     iota(R("m8"), [[0, 64]], 1)
@@ -186,6 +186,7 @@ def rank_program(g, core, T, topo):
     op("g", lambda: g.affine_select(T.et[:], T.ones[:], [[-1, 516]], A.is_equal, 0.0, 3, 4), [R("ones")], [R("et")])
 
     fill(R("zero"), 0.0)
+    fill(R("kin"), 0.0)
     act(R("kt", 2, 1040, 4), R("zero"))
     act(R("kt", 3, 1040, 4), R("zero"))
     act(R("kt", 512, 1040, 520), R("zero", 0, 2))
@@ -193,32 +194,32 @@ def rank_program(g, core, T, topo):
     act(R("st", 3, 512, 4), R("zero", 0, 128))
     for c, sh in enumerate([3, 2, 1, 0, 4]):
         ts(col("ib", c), col("pi", 0), sh, 1, A.logical_shift_right, A.bitwise_and)
-    fill(R("kin"), 0.0)
-    cp(R("fb", 0, 5), R("ib", 0, 5))
     ts(col("ib", 5), col("pi", 0), 3, None, A.bitwise_and)
+    cp(R("fb", 0, 5), R("ib", 0, 5))
+    ts(col("ib", 6), col("pi", 0), 2, 3, A.logical_shift_right, A.bitwise_and)
+    ts(col("ib", 7), col("pi", 0), 15, None, A.bitwise_and)
     ts(R("fb", 12, 16), R("fb", 0, 4), 2.0, -1.0, A.mult, A.add)
     ts(col("fb", 16), col("fb", 4), -1.0, 1.0, A.mult, A.add)
-    ts(col("ib", 6), col("pi", 0), 2, 3, A.logical_shift_right, A.bitwise_and)
+    ts(col("ib", 8), col("pi", 0), 7, None, A.bitwise_and)
     ts(R3("ksrc", 1, s(0, 4)), R("fb", 12, 16), col("fb", 4), None, A.mult)
     ts(R3("ksrc", 0, s(0, 4)), R("fb", 12, 16), col("fb", 16), None, A.mult)
     op("v", lambda: V.tensor_reduce(T.fb[:, 17:18], T.fb[:, 0:4], AxisListType.X, A.add), [R("fb", 0, 4)], [col("fb", 17)])
+    ts(col("fb", 18), col("fb", 16), -10.0, 1.0, A.mult, A.add)
     for a in range(4):
         cp(N("kin", s(32 * a, 32 * a + 32), s(0, 2), s(16 + 32 * a, 20 + 32 * a)), N("ksrc", s(32 * a, 32 * a + 32), s(0, 2), s(0, 4)))
-    ts(col("ib", 7), col("pi", 0), 15, None, A.bitwise_and)
+    cp(R("fb", 5, 9), R("ib", 5, 9))
+    tt(col("fb", 19), col("fb", 18), col("fb", 17), A.subtract)
     for y in range(2):
         for var in range(2):
             tr(R("kt", 520 * y + var, 520 * y + 512, 4), R3("kin", var, s(16 - 16 * y, 144 - 16 * y)))
-    ts(col("ib", 8), col("pi", 0), 7, None, A.bitwise_and)
     for y in range(2):
         quant("k", 128 * y, R("kt", 520 * y, 520 * y + 512))
     quant("u", 0, R("us"))
 
     def constants_1():
-        ts(col("fb", 18), col("fb", 16), -10.0, 1.0, A.mult, A.add)
-        cp(R("fb", 5, 9), R("ib", 5, 9))
-        tt(col("fb", 19), col("fb", 18), col("fb", 17), A.subtract)
         cp(R3("ab", s(0, 4), s(129, 145)), R("zero", 0, 64))
         cp(R3("ab", s(0, 4), s(0, 1)), R("zero", 0, 4))
+        cp(R("wk", 31, 576, 32), R("zero", 0, 18))
 
     def ramps():
         tt(R3("dd", s(0, 2), s(0, 32)), R3("cd", s(0, 2), s(0, 32)), R3("cd", s(0, 2), s(1, 33)), A.subtract)
@@ -242,16 +243,16 @@ def rank_program(g, core, T, topo):
         lambda: ts(col("ib", 9), col("pi", 0), 1, 7, A.logical_shift_right, A.bitwise_and),
         lambda: ts(R("lj"), R("fb", 10, 12), col("fb", 9), col("fb", 8), A.mult, A.add),
         lambda: cp(col("fb", 24), col("ib", 9)),
-        lambda: ts(R("mk"), R("k8"), col("fb", 24), None, A.is_equal),
         lambda: ts(col("fb", 25), col("fb", 3), 2.0, col("fb", 5), A.mult, A.subtract),
+        lambda: ts(R("mk"), R("k8"), col("fb", 24), None, A.is_equal),
     ]
 
     def gap():
         if small:
             small.pop(0)()
 
-    def pen(a, c):
-        ts(R("pen", a, 512, c), R("w", a, 512, c), BIG, -BIG, A.is_gt, A.mult)
+    def pen(a, c, src, lim):
+        ts(R("pen", a, 512, c), src, lim, -BIG, A.is_gt, A.mult)
 
     def knock(a, c):
         scan(R("wk", a, 512, c), R("pen", a, 512, c), R("w", a, 512, c), 0.0, A.min, A.add)
@@ -277,8 +278,7 @@ def rank_program(g, core, T, topo):
             act(R(xw, 1024, 2048), R(xo))
         for y in range(2):
             ts(R3("ab", y, s(1, 129)), PS(2 + y), col("fb", 17), -BIG, A.is_equal, A.mult)
-        for y in range(2):
-            ts(R3("ab", 2 + y, s(1, 129)), R3("ab", y, s(1, 129)), -(1.0 + 1.0 / BIG), None, A.mult)
+            ts(R3("ab", 2 + y, s(1, 129)), PS(2 + y), col("fb", 17), BIG + 1.0, A.is_equal, A.mult)
         for y in range(2):
             scan(R3("cs", y, s(0, 144)), R3("ab", y, s(0, 144)), R3("ab", 2 + y, s(1, 145)), col("car", y), A.add, A.add)
         for y in range(2):
@@ -289,45 +289,46 @@ def rank_program(g, core, T, topo):
         if t == 0:
             act(R(xw, 1024, 2048), R(xo))
         scan(R("in3"), R("mz"), R("w", 0, 576, 2), 0.0, A.mult, A.add)
+        pen(0, 2, R("w", 0, 512, 2), BIG)
         gap()
-        pen(0, 2)
         ts(R("w", 1, 576, 4), R("in3", 1, 288, 2), -8.0, 0.0, A.add, A.max)
         gap()
         knock(0, 2)
         scan(R("in2"), R("mz", 0, 144), R("w", 1, 576, 4), 0.0, A.mult, A.add)
         gap()
-        pen(1, 4)
+        pen(1, 4, R("w", 1, 512, 4), BIG)
+        gap()
         ts(R("w", 3, 576, 8), R("in2", 1, 144, 2), -8.0, 0.0, A.add, A.max)
-        ts(R("dl", 5, 8), R("in2", 137, 142, 2), 8.0, None, A.min)
-        tt(R("in1"), R("w", 3, 576, 16), R("w", 11, 576, 16), A.add)
-        gap()
+        pen(3, 8, R("in2", 1, 128, 2), BIG + 8.0)
         knock(1, 4)
+        tt(R("in1"), R("w", 3, 576, 16), R("w", 11, 576, 16), A.add)
+        knock(3, 8)
+        ts(R("dl", 5, 8), R("in2", 137, 142, 2), 8.0, None, A.min)
         ts(R("w", 7, 576, 16), R("in1"), -8.0, 0.0, A.add, A.max)
+        pen(7, 16, R("in1", 0, 32), BIG + 8.0)
         ts(R("dl", 3, 5), R("in1", 34, 36), 8.0, None, A.min)
-        tt(R("in0"), R("w", 7, 576, 32), R("w", 23, 576, 32), A.add)
+        tt(R("wk", 15, 576, 32), R("w", 7, 576, 32), R("w", 23, 576, 32), A.add)
+        knock(7, 16)
         gap()
-        ts(R("w", 15, 512, 32), R("in0", 0, 16), -8.0, None, A.add)
-        ts(R("w", 31, 512, 32), R("in0", 0, 16), -608.0, None, A.add)
-        ts(col("dl", 1), col("in0", 17), -8.0, None, A.add)
-        pen(3, 4)
+        gap()
+        scan(R("sp"), R3("dd", 0, s(0, 512)), R("wk", 0, 512), 0.0, A.add, A.max)
+        ts(col("dl", 1), col("wk", 559), -8.0, None, A.add)
+        scan(R("sm"), R3("dd", 1, s(0, 512)), R("wk", 0, 512), 0.0, A.add, A.max)
+        ts(R("opos"), R("sp", 31, 512, 32), 7.0 - BIG, None, A.add)
         scan(R("th"), R("dl"), R("dl"), 0.0, A.add, A.max)
-        knock(3, 4)
-        tt(R("dj", 1, 8), R("da", 1, 8), R("dl", 1, 8), A.subtract)
-        scan(R("sp"), R3("dd", 0, s(0, 512)), R("wk"), 0.0, A.add, A.max)
-        scan(R("sm"), R3("dd", 1, s(0, 512)), R("wk"), 0.0, A.add, A.max)
-        ts(R("opos"), R("sp", 31, 512, 32), -425.0, None, A.add)
         for h in range(2):
-            ts(R("omp", 8 * h, 8 * h + 8), R("sm", 31 + 32 * h, 512, 64), -425.0, 248.0, A.add, A.max)
+            ts(R("omp", 8 * h, 8 * h + 8), R("sm", 31 + 32 * h, 512, 64), 7.0 - BIG, None, A.add)
         scatter(R(tab), R("opos"), R("val"))
         tt(R("cmp"), R("th"), R("kc"), A.is_le, off=R("lt"))
+        tt(R("dj", 1, 8), R("da", 1, 8), R("dl", 1, 8), A.subtract)
         tt(R("mm"), R(tab), R("own"), A.min, off=R("omp"))
         tt(R("prod"), R("dj"), R("cmp"), A.mult, off=R("lj"))
+        gap()
         scan(R("mx4"), R("s4"), R("mm"), 0.0, A.add, A.max)
         scan(R("s8"), R("m8", 0, 32), R("prod"), 0.0, A.mult, A.add)
+        gap()
         ts(R("oz"), R("mx4", 3, 256, 4), 1024.0, None, A.add)
         ts(R("oi"), R("s8", 7, 32, 8), col("fb", 7), None, A.add)
-        gap()
-        gap()
         for h in range(2):
             tt(R("zt", 512 * h, 512 * h + 512), R(xw), R(xo, 512 * h, 512 * h + 512), A.add, off=R("oz", 32 * h, 32 * h + 32))
             if h == 0:
@@ -340,7 +341,6 @@ def rank_program(g, core, T, topo):
             if h == 0:
                 for b in range(4):
                     act(R(xn, b, 512, 4), PS(b), scale=0.015625)
-        gap()
         if t == 0:
             quant(ln, 128, R("zero2"))
         for k in range(2):
@@ -368,14 +368,15 @@ def rank_program(g, core, T, topo):
             for b in (0, 2, 1, 3):
                 quant("e", 128 * b, R("et", 3 - b, 515 - b))
         if t == 1:
-            iota(R("att", 0, 256), [[0, 256]], -1)
+            iota(R("att", 0, 16), [[0, 16]], 0)
+            iota(R("att", 16, 256), [[0, 240]], -1)
             iota(R("att", 256, 512), [[1, 32], [0, 8]], 0)
             quant("v", 0, R("vs"))
         if t < ROUNDS - 1:
             quant("l%d" % (t + 1), 128, R("zero2"))
         else:
             for h in range(2):
-                ts(R("onat", 8 * h, 8 * h + 8), R("sp", 31 + 32 * h, 512, 64), -425.0, None, A.add)
+                ts(R("onat", 8 * h, 8 * h + 8), R("sp", 31 + 32 * h, 512, 64), 7.0 - BIG, None, A.add)
             act(R("atr"), R("att"), off=R("onat"))
             store("s", T.ob[:], N("atr", s(0, 128, 16), s(0, 256)))
         for b in (0, 2, 1, 3):

@@ -9,10 +9,10 @@ BIG = 1024.0
 SCRATCH = {}
 for _d, _l in {
     "bfloat16": dict(us=512, vs=512, kt=1040, kin=[2, 144], et=516, ones=516, zero=260, zero2=512, st=512, bt=512, zt=1024, came=256, junk=256,
-                     dd=[2, 512], mz=288, s4=256, x0=1024, x1=1024, x2=1024, x3=1024, xw0=2048, xw1=2048, xw2=2048),
+                     dd=[2, 512], p4=576, p6=432, s4=256, x0=1024, x1=1024, x2=1024, x3=1024, xw0=2048, xw1=2048, xw2=2048),
     "float8_e4m3fn_x4": dict(qu=128, qv=128, qw=512, qx=256, qz=256, qs=128, qk=512, qe=512, ql0=320, ql1=320, ql2=320),
     "uint8": dict(su=128, sv=128, sw=512, sx=256, sz=256, ss=128, sk=512, se=512, sl0=512, sl1=512, sl2=512),
-    "float16": dict(ab=[4, 146], cs=[2, 144], d4=[9, 2, 16], w=576, in3=288, in2=144, in1=36, pen=512, wk=576, sp=512, sm=512,
+    "float16": dict(ab=[4, 146], cs=[2, 144], d4=[9, 2, 16], lv=576, o3=1728, o2=432, in1=36, o1=36, c2=4, pen=512, wk=576, sp=512, sm=512,
                     mm=256, mx4=256),
     "float32": dict(ksrc=[2, 4], fb=26, car=2, cd=[2, 33], m8=64, k8=64, mk=64, me=64, me8=64, val=256, val0=256, own=256, own0=256, own1=256,
                     dl=8, da=8, th=8, dj=16, kc=32, kc0=32, cmp=32, prod=32, s8=32, i4=4, att=512, atr=256, ys=256, tab0=512, tab1=512, tab2=512),
@@ -169,7 +169,6 @@ def rank_program(g, core, T, topo):
     iota(R("val0"), [[64, 8], [512, 2], [4, 16]], -1024)
     iota(R("own0"), [[4, 256]], 4096)
     iota(R("kc0"), [[16, 4], [0, 8]], 0)
-    iota(R("mz"), [[0, 144], [1, 2]], 0)
     iota(R("dl", 0, 3), [[4, 3]], 0)
     iota(R("da", 3, 8), [[0, 5]], 8)
     iota(R("da", 1, 3), [[264, 2]], -8)
@@ -192,15 +191,21 @@ def rank_program(g, core, T, topo):
     act(R("kt", 512, 1040, 520), R("zero", 0, 2))
     act(R("st", 2, 512, 4), R("zero", 0, 128))
     act(R("st", 3, 512, 4), R("zero", 0, 128))
+    for n, w in (("p4", 4), ("p6", 6)):
+        for k in range(w):
+            c = -8.0 if k == 0 else 0.0 if k == w - 1 else -4096.0
+            act(R(n, k, None, w), R("zero", 0, 144 if w == 4 else 72), F.Identity, bias=c)
     for c, sh in enumerate([3, 2, 1, 0, 4]):
         ts(col("ib", c), col("pi", 0), sh, 1, A.logical_shift_right, A.bitwise_and)
     ts(col("ib", 5), col("pi", 0), 3, None, A.bitwise_and)
-    cp(R("fb", 0, 5), R("ib", 0, 5))
     ts(col("ib", 6), col("pi", 0), 2, 3, A.logical_shift_right, A.bitwise_and)
     ts(col("ib", 7), col("pi", 0), 15, None, A.bitwise_and)
-    ts(R("fb", 12, 16), R("fb", 0, 4), 2.0, -1.0, A.mult, A.add)
-    ts(col("fb", 16), col("fb", 4), -1.0, 1.0, A.mult, A.add)
+    ts(R("fb", 12, 16), R("ib", 0, 4), 2.0, -1.0, A.mult, A.add)
+    cp(R("fb", 0, 5), R("ib", 0, 5))
+    ts(col("fb", 16), col("ib", 4), -1.0, 1.0, A.mult, A.add)
     ts(col("ib", 8), col("pi", 0), 7, None, A.bitwise_and)
+    for k, c in ((0, -8192.0), (2, 0.0)):
+        ts(R("lv", k, 576, 4), R("zero", 0, 144), c, None, A.add)
     ts(R3("ksrc", 1, s(0, 4)), R("fb", 12, 16), col("fb", 4), None, A.mult)
     ts(R3("ksrc", 0, s(0, 4)), R("fb", 12, 16), col("fb", 16), None, A.mult)
     op("v", lambda: V.tensor_reduce(T.fb[:, 17:18], T.fb[:, 0:4], AxisListType.X, A.add), [R("fb", 0, 4)], [col("fb", 17)])
@@ -212,14 +217,15 @@ def rank_program(g, core, T, topo):
     for y in range(2):
         for var in range(2):
             tr(R("kt", 520 * y + var, 520 * y + 512, 4), R3("kin", var, s(16 - 16 * y, 144 - 16 * y)))
-    for y in range(2):
-        quant("k", 128 * y, R("kt", 520 * y, 520 * y + 512))
+    quant("k", 0, R("kt", 0, 512))
     quant("u", 0, R("us"))
 
     def constants_1():
         cp(R3("ab", s(0, 4), s(129, 145)), R("zero", 0, 64))
         cp(R3("ab", s(0, 4), s(0, 1)), R("zero", 0, 4))
         cp(R("wk", 31, 576, 32), R("zero", 0, 18))
+        for k, c in ((1, -8192.0), (5, 0.0), (13, 0.0), (17, 0.0)):
+            ts(R("o3", k, 1728, 24), R("zero", 0, 72), c, None, A.add)
 
     def ramps():
         tt(R3("dd", s(0, 2), s(0, 32)), R3("cd", s(0, 2), s(0, 32)), R3("cd", s(0, 2), s(1, 33)), A.subtract)
@@ -242,8 +248,8 @@ def rank_program(g, core, T, topo):
         lambda: ts(R("fb", 10, 12), R("i4", 0, 4, 2), col("fb", 0), 8.0, A.add, A.add),
         lambda: ts(col("ib", 9), col("pi", 0), 1, 7, A.logical_shift_right, A.bitwise_and),
         lambda: ts(R("lj"), R("fb", 10, 12), col("fb", 9), col("fb", 8), A.mult, A.add),
-        lambda: cp(col("fb", 24), col("ib", 9)),
         lambda: ts(col("fb", 25), col("fb", 3), 2.0, col("fb", 5), A.mult, A.subtract),
+        lambda: cp(col("fb", 24), col("ib", 9)),
         lambda: ts(R("mk"), R("k8"), col("fb", 24), None, A.is_equal),
     ]
 
@@ -254,18 +260,21 @@ def rank_program(g, core, T, topo):
     def pen(a, c, src, lim):
         ts(R("pen", a, 512, c), src, lim, -BIG, A.is_gt, A.mult)
 
-    def knock(a, c):
-        scan(R("wk", a, 512, c), R("pen", a, 512, c), R("w", a, 512, c), 0.0, A.min, A.add)
+    def knock(a, c, src):
+        scan(R("wk", a, 512, c), R("pen", a, 512, c), src, 0.0, A.min, A.add)
 
     for t in range(ROUNDS):
         xn, xo, xw, tab, ln = "x%d" % (t + 1), "x%d" % t, "xw%d" % t, "tab%d" % t, "l%d" % t
         for h in range(2):
             quant("x", 128 * h, R(xo, 512 * h, 512 * h + 512))
             mm(h, "u", 0, "x", 128 * h)
+        if t == 0:
+            quant("k", 128, R("kt", 520, 1032))
+            quant("k", 256, R("kt", 1, 513))
         for h in range(2):
-            if t == 0:
-                quant("k", 256 + 128 * h, R("kt", 520 * h + 1, 520 * h + 513))
             ts(R("st", h, 512, 4), PS(h), 0.0, None, A.is_ge)
+        if t == 0:
+            quant("k", 384, R("kt", 521, 1033))
         quant("s", 0, R("st"))
         if t == 0:
             constants_1()
@@ -284,63 +293,71 @@ def rank_program(g, core, T, topo):
         for y in range(2):
             ts(R3("d4", s(0, 9), y, s(0, 16)), R3("cs", y, s(0, 144)), -8.0, 0.0, A.add, A.max)
         gap()
-        tr(R("w", 0, 576, 2), R("d4"))
+        tr(R("lv", 1, 576, 2), R("d4"))
         gap()
         if t == 0:
             act(R(xw, 1024, 2048), R(xo))
-        scan(R("in3"), R("mz"), R("w", 0, 576, 2), 0.0, A.mult, A.add)
-        pen(0, 2, R("w", 0, 512, 2), BIG)
+        scan(R("o3", 0, 1728, 3), R("lv"), R("p4"), 0.0, A.add, A.max)
+        pen(0, 2, R("lv", 1, 512, 2), BIG)
         gap()
-        ts(R("w", 1, 576, 4), R("in3", 1, 288, 2), -8.0, 0.0, A.add, A.max)
         gap()
-        knock(0, 2)
-        scan(R("in2"), R("mz", 0, 144), R("w", 1, 576, 4), 0.0, A.mult, A.add)
+        scan(R("o2"), R("o3", 1, 1728, 4), R("p6"), 0.0, A.add, A.max)
+        knock(0, 2, R("lv", 1, 512, 2))
+        pen(1, 4, R("o3", 9, 1536, 12), BIG)
+        tt(R("c2", 0, 3), R("o3", 1641, 1700, 24), R("o3", 1653, 1710, 24), A.add)
+        tt(R("in1"), R("o2", 5, 432, 12), R("o2", 11, 432, 12), A.add)
+        pen(3, 8, R("o2", 5, 384, 6), BIG)
+        ts(R("dl", 5, 8), R("c2", 0, 3), 8.0, None, A.min)
+        knock(1, 4, R("o3", 9, 1536, 12))
         gap()
-        pen(1, 4, R("w", 1, 512, 4), BIG)
-        gap()
-        ts(R("w", 3, 576, 8), R("in2", 1, 144, 2), -8.0, 0.0, A.add, A.max)
-        pen(3, 8, R("in2", 1, 128, 2), BIG + 8.0)
-        knock(1, 4)
-        tt(R("in1"), R("w", 3, 576, 16), R("w", 11, 576, 16), A.add)
-        knock(3, 8)
-        ts(R("dl", 5, 8), R("in2", 137, 142, 2), 8.0, None, A.min)
-        ts(R("w", 7, 576, 16), R("in1"), -8.0, 0.0, A.add, A.max)
+        ts(R("o1"), R("in1"), -8.0, 0.0, A.add, A.max)
         pen(7, 16, R("in1", 0, 32), BIG + 8.0)
+        knock(3, 8, R("o2", 5, 384, 6))
         ts(R("dl", 3, 5), R("in1", 34, 36), 8.0, None, A.min)
-        tt(R("wk", 15, 576, 32), R("w", 7, 576, 32), R("w", 23, 576, 32), A.add)
-        knock(7, 16)
+        gap()
+        tt(R("wk", 15, 576, 32), R("o1", 0, 36, 2), R("o1", 1, 36, 2), A.add)
+        knock(7, 16, R("o1", 0, 32))
         gap()
         gap()
         scan(R("sp"), R3("dd", 0, s(0, 512)), R("wk", 0, 512), 0.0, A.add, A.max)
-        ts(col("dl", 1), col("wk", 559), -8.0, None, A.add)
         scan(R("sm"), R3("dd", 1, s(0, 512)), R("wk", 0, 512), 0.0, A.add, A.max)
         ts(R("opos"), R("sp", 31, 512, 32), 7.0 - BIG, None, A.add)
-        scan(R("th"), R("dl"), R("dl"), 0.0, A.add, A.max)
+        ts(col("dl", 1), col("wk", 559), -8.0, None, A.add)
         for h in range(2):
             ts(R("omp", 8 * h, 8 * h + 8), R("sm", 31 + 32 * h, 512, 64), 7.0 - BIG, None, A.add)
         scatter(R(tab), R("opos"), R("val"))
-        tt(R("cmp"), R("th"), R("kc"), A.is_le, off=R("lt"))
+        scan(R("th"), R("dl"), R("dl"), 0.0, A.add, A.max)
         tt(R("dj", 1, 8), R("da", 1, 8), R("dl", 1, 8), A.subtract)
-        tt(R("mm"), R(tab), R("own"), A.min, off=R("omp"))
-        tt(R("prod"), R("dj"), R("cmp"), A.mult, off=R("lj"))
         gap()
-        scan(R("mx4"), R("s4"), R("mm"), 0.0, A.add, A.max)
-        scan(R("s8"), R("m8", 0, 32), R("prod"), 0.0, A.mult, A.add)
-        gap()
-        ts(R("oz"), R("mx4", 3, 256, 4), 1024.0, None, A.add)
-        ts(R("oi"), R("s8", 7, 32, 8), col("fb", 7), None, A.add)
         for h in range(2):
-            tt(R("zt", 512 * h, 512 * h + 512), R(xw), R(xo, 512 * h, 512 * h + 512), A.add, off=R("oz", 32 * h, 32 * h + 32))
-            if h == 0:
-                tt(R("me"), R(tab), R("mk"), A.mult, off=R("oi"))
-            else:
-                scan(R("me8"), R("m8"), R("me"), 0.0, A.mult, A.add)
+            tt(R("mm", 128 * h, 128 * h + 128), R(tab), R("own", 128 * h, 128 * h + 128), A.min, off=R("omp", 8 * h, 8 * h + 8))
+        scan(R("mx4", 0, 128), R("s4", 0, 128), R("mm", 0, 128), 0.0, A.add, A.max)
+        tt(R("cmp"), R("th"), R("kc"), A.is_le, off=R("lt"))
+        gap()
+        scan(R("mx4", 128, 256), R("s4", 0, 128), R("mm", 128, 256), 0.0, A.add, A.max)
+        ts(R("oz", 0, 32), R("mx4", 3, 128, 4), 1024.0, None, A.add)
+        tt(R("prod"), R("dj"), R("cmp"), A.mult, off=R("lj"))
+        ts(R("oz", 32, 64), R("mx4", 131, 256, 4), 1024.0, None, A.add)
+
+        def meet(a, b):
+            tt(R("zt", 16 * a, 16 * b), R(xw), R(xo, 16 * a, 16 * b), A.add, off=R("oz", a, b))
+
+        def layer(h):
             quant("z", 128 * h, R("zt", 512 * h, 512 * h + 512))
             for b in range(4):
                 mm(4 * h + b, "w", 128 * b, "z", 128 * h)
-            if h == 0:
-                for b in range(4):
-                    act(R(xn, b, 512, 4), PS(b), scale=0.015625)
+
+        meet(0, 32)
+        scan(R("s8"), R("m8", 0, 32), R("prod"), 0.0, A.mult, A.add)
+        meet(32, 40)
+        layer(0)
+        for b in range(4):
+            act(R(xn, b, 512, 4), PS(b), scale=0.015625)
+        ts(R("oi"), R("s8", 7, 32, 8), col("fb", 7), None, A.add)
+        meet(40, 64)
+        tt(R("me"), R(tab), R("mk"), A.mult, off=R("oi"))
+        layer(1)
+        scan(R("me8"), R("m8"), R("me"), 0.0, A.mult, A.add)
         if t == 0:
             quant(ln, 128, R("zero2"))
         for k in range(2):
@@ -381,9 +398,8 @@ def rank_program(g, core, T, topo):
             store("s", T.ob[:], N("atr", s(0, 128, 16), s(0, 256)))
         for b in (0, 2, 1, 3):
             mm(b, "e", 128 * b, ln, 192)
-            (act if b % 2 else cp)(R("came", 128 * (b % 2) + b // 2, 128 * (b % 2) + 128, 2), PS(b, 64))
-        for k in range(2):
-            scatter(R(xn), R("oe", 8 * k, 8 * k + 8), R("came", 128 * k, 128 * k + 128))
+            cp(R("came", 128 * (b % 2) + b // 2, 128 * (b % 2) + 128, 2), PS(b, 64))
+        scatter(R(xn), R("oe"), R("came"))
 
     for h in range(2):
         quant("x", 128 * h, R("x%d" % ROUNDS, 512 * h, 512 * h + 512))

@@ -1,30 +1,33 @@
 import numpy as np
 from concourse.bass import DstId, RemoteDMATransfer
-from concourse.mybir import dt, AluOpType, AxisListType, ActivationFunctionType
+from concourse.mybir import dt, AluOpType, ActivationFunctionType
 
 A = AluOpType
 F = ActivationFunctionType
 ROUNDS = 3
-BIG = 1024.0
+U = 2.0 ** -10
+EMPTY = 512
 SCRATCH = {}
 for _d, _l in {
-    "bfloat16": dict(us=512, vs=512, kt=1040, kin=[2, 144], et=516, ones=516, zero=260, zero2=512, st=512, bt=512, zt=1024, came=256, junk=256,
-                     dd=[2, 512], p4=576, p6=432, s4=256, x0=1024, x1=1024, x2=1024, x3=1024, xw0=2048, xw1=2048, xw2=2048),
-    "float8_e4m3fn_x4": dict(qu=128, qv=128, qw=512, qx=256, qz=256, qs=128, qk=512, qe=512, ql0=320, ql1=320, ql2=320),
-    "uint8": dict(su=128, sv=128, sw=512, sx=256, sz=256, ss=128, sk=512, se=512, sl0=512, sl1=512, sl2=512),
-    "float16": dict(ab=[4, 146], cs=[2, 144], d4=[9, 2, 16], lv=576, o3=1728, o2=432, in1=36, o1=36, c2=4, pen=512, wk=576, sp=512, sm=512,
-                    mm=256, mx4=256),
-    "float32": dict(ksrc=[2, 4], fb=26, car=2, cd=[2, 33], m8=64, k8=64, mk=64, me=64, me8=64, val=256, val0=256, own=256, own0=256, own1=256,
-                    dl=8, da=8, th=8, dj=16, kc=32, kc0=32, cmp=32, prod=32, s8=32, i4=4, att=512, atr=256, ys=256, tab0=512, tab1=512, tab2=512),
-    "int32": dict(pi=2, ib=10),
-    "uint16": dict(opos=16, omp=16, oz=64, oi=4, oe=16, onat=16, lt=2, lj=2),
+    "bfloat16": dict(us=512, vs=512, kt=1088, kin=[2, 144], et=516, ones=516, zero=512, st=512, zt=1024, junk=512,
+                     ab0=[2, 128], s4=512, s6=384, p4=512, p6=384, dd=[2, 512], pen=448, val=256, row=256, tab0=528, tab1=528, tab2=528,
+                     sg=128, cum=128, lin=128, mk=64, k16=64, m16=64, me=64, me16=64, att=528, sel=256, mr=64,
+                     xw0=2048, xw1=2048, xw2=2048, yw0=2048, yw1=2048, yw2=2048, x0=1024, x1=1024, x2=1024, x3=1024),
+    "float8_e4m3fn_x4": dict(qu=128, qv=128, qw=512, qx=256, qz=256, qs=128, qk=272, qe=512, qy0=256, qy1=256, qy2=256, ql0=256, ql1=256, ql2=256),
+    "uint8": dict(su=128, sv=128, sw=512, sx=256, sz=256, ss=128, sk=272, se=512, sy0=256, sy1=256, sy2=256, sl0=256, sl1=256, sl2=256),
+    "float16": dict(ab1=[2, 128], cs=[2, 128], d4=256, lv=512, o3=1536, o2=384, wk=512, sp=512, sm=512, mm=256, mx4=256, mx2=256),
+    "float32": dict(ksrc=[2, 4], fb=32, car=2, acc=4, lrow=8, cd=[2, 33], own=256, mp=256, new=64, atr=256, ys=256),
+    "int32": dict(pi=2, ib=6),
+    "uint16": dict(opos=16, omp=16, onat=16, oz=64, ox=64, oi=4, oe0=4, oe1=4, oe2=4, le0=8, le1=8, le2=8, lo=8),
 }.items():
     for _n, _s in _l.items():
         SCRATCH[_n] = ("sbuf", [128] + (_s if isinstance(_s, list) else [_s]), _d)
+SCRATCH["d4"] = ("sbuf", [128, 8, 2, 16], "float16")
 for _t in range(8):
     SCRATCH["ps%d" % _t] = ("psum", [128, 512], "float32")
 
-SEMAPHORES = ["v", "a", "p", "g", "ldx", "ldy", "ldu", "ldw", "lds", "ldv", "ld0", "sent0", "sent1", "sent2", "arr0", "arr1", "arr2", "out"]
+SEMAPHORES = ["v", "a", "p", "g", "ldx", "ldy", "ldu", "ldw", "lds", "ldv", "win0", "win1", "sent", "out"] + [
+    "%s%d" % (_n, _t) for _n in ("lst", "one", "two") for _t in range(ROUNDS)]
 
 
 def rank_program(g, core, T, topo):
@@ -41,6 +44,7 @@ def rank_program(g, core, T, topo):
     known = {e: {} for e in Q}
     log = {}
     s = slice
+    ALL = s(None)
 
     def N(name, *idx):
         where, shape, _d = SCRATCH[name]
@@ -117,24 +121,30 @@ def rank_program(g, core, T, topo):
     def fill(out, c):
         op("v", lambda: V.memset(out[0], c), [], [out])
 
-    def quant(n, a, in_):
-        q, sc = R("q" + n, a, a + 128), R("s" + n, a, a + 128)
+    def quant(n, a, in_, w=128):
+        q, sc = R("q" + n, a, a + w), R("s" + n, a, a + w)
         op("v", lambda: V.quantize_mx(q[0], sc[0], in_[0]), [in_], [q, sc])
 
-    def PS(bank, a=0):
-        return R("ps%d" % bank, a, 128)
+    def PS(bank, n=128):
+        return R("ps%d" % bank, 0, n)
 
     def mm(bank, w, wa, x, xa):
         o, a, b, c, d = PS(bank), R("q" + w, wa, wa + 128), R("s" + w, wa, wa + 128), R("q" + x, xa, xa + 128), R("s" + x, xa, xa + 128)
         op("p", lambda: g.tensor.matmul_mx(o[0], a[0], b[0], c[0], d[0], True, True), [a, b, c, d], [o])
 
-    def act(out, in_, fn=F.Copy, bias=None, scale=1.0, acc=None, off=None):
+    def act(out, in_, fn=F.Identity, bias=None, scale=1.0, acc=None, off=None):
         kw = {"scale": ap(scale)}
         if bias is not None:
             kw["bias"] = ap(bias)
         if acc:
             kw["accum_out"] = acc[0]
         op("a", lambda: g.scalar.activation(out[0], ap(in_, off), fn, **kw), [in_, bias, scale, off], [out] + ([acc] if acc else []))
+
+    def out_of_psum(e, dst, bank, scale):
+        if e == "a":
+            act(dst, PS(bank), F.Copy, scale=scale)
+        else:
+            ts(dst, PS(bank), scale, None, A.mult)
 
     def iota(out, pat, base):
         op("g", lambda: g.iota(out[0], pat, base, 0, allow_small_or_imprecise_dtypes=True), [], [out])
@@ -150,265 +160,247 @@ def rank_program(g, core, T, topo):
         Q[e].dma_start(dst, u8(src)).then_inc(T.sem.out, 16)
         count["out"] = count.get("out", 0) + 16
 
+    def send(sem, calls):
+        for call in calls:
+            order("g", [c[0] for c in call], [])
+            g.remote_dma_fused([RemoteDMATransfer(dst_ids=[DstId(rid=rid, pnc=pid)], dma_engine_mask=sum(1 << e for e in es),
+                                                  remote_sem=T.sem[sem], src=u8(src), dst=u8(dst)) for src, dst, es in call], local_sem=T.sem.sent)
+            for k in (sem, "sent"):
+                count[k] = count.get(k, 0) + sum(len(c[2]) for c in call)
+        note((sem, count[sem], {}), [], [c[1] for call in calls for c in call])
+
+    def X(t, a=0, b=1024, c=None):
+        return R("x%d" % t, a, b, c)
+
     load("a", R("us"), T.u[:], "ldu")
-    load("s", R("x0", 0, 512), T.x[:, 0:512], "ldx")
-    wait("s", load("s", R("x0", 512, 1024), T.x[:, 512:1024], "ldy"))
+    load("s", X(0, 0, 512), T.x[:, 0:512], "ldx")
+    wait("s", load("s", X(0, 512, 1024), T.x[:, 512:1024], "ldy"))
     load("s", R("qw"), T.wc[:], "ldw")
     load("s", R("sw"), T.ws[:], "lds")
-    load("s", R("xw0", 0, 1024), T.x[:], "ld0")
-    load("s", R("vs"), T.v[:], "ldv")
+    load("s", R("xw0", 0, 1024), T.x[:], "win0")
 
     op("g", lambda: g.iota(T.pi[:, 0:1], [[0, 1]], 0, 1), [], [col("pi", 0)])
-    for k, (pats, bases) in enumerate([([[[8, 16]], [[8, 8]], [[8, 4]], [[8, 2]]], [383, 319, 287, 271]),
-                                       ([[[8, 8], [0, 2]], [[8, 4], [0, 2]], [[8, 2], [0, 2]], [[0, 2]]], [319, 287, 271, 15])]):
+    iota(R3("ab0", ALL, s(0, 1)), [[0, 2]], 0)
+    iota(R("s4"), [[0, 128], [1024, 4]], 0)
+    iota(R("s6"), [[0, 64], [1024, 6]], 0)
+    for k, (pats, bases) in enumerate([([[[8, 16]], [[8, 8]], [[8, 4]], [[64, 2]]], [407, 335, 287, 183]),
+                                       ([[[8, 8], [0, 2]], [[8, 4], [0, 2]], [[64, 2], [0, 2]], [[0, 2]]], [343, 303, 215, -41])]):
         for lv in range(4):
             iota(R3("cd", k, s(1 << lv, 33 if lv else 32, 2 << lv)), pats[lv], bases[lv])
-    iota(R3("cd", s(0, 2), s(0, 33, 32)), [[0, 2], [2007, 2]], -2000)
-    iota(R3("cd", s(0, 2), s(16, 17)), [[-304, 2]], 7)
-    iota(R("i4"), [[1, 4]], 0)
-    iota(R("val0"), [[64, 8], [512, 2], [4, 16]], -1024)
-    iota(R("own0"), [[4, 256]], 4096)
-    iota(R("kc0"), [[16, 4], [0, 8]], 0)
-    iota(R("dl", 0, 3), [[4, 3]], 0)
-    iota(R("da", 3, 8), [[0, 5]], 8)
-    iota(R("da", 1, 3), [[264, 2]], -8)
-    iota(R("dj"), [[0, 4], [16, 4]], 16)
-    iota(R("tab0"), [[0, 512]], 4096)
-    iota(R("s4"), [[0, 256]], 0)
-    iota(R("m8"), [[0, 64]], 1)
-    iota(R("k8"), [[0, 8], [1, 8]], 0)
-    iota(R("s4", 0, 256, 4), [[0, 64]], -8192)
-    iota(R("m8", 0, 64, 8), [[0, 8]], 0)
-    iota(R("bt", 256, 512), [[0, 256]], 0)
-    iota(R("zero2"), [[0, 512]], 0)
+    iota(R3("cd", ALL, s(16, 33, 16)), [[-552, 2], [56, 2]], -105)
+    iota(R3("cd", ALL, s(0, 1)), [[-64, 2]], -1633)
+    iota(R("lrow"), [[264, 2], [16, 4]], 16)
+    iota(R("val"), [[16, 8], [128, 2], [1, 16]], 0)
+    iota(R("row"), [[1, 256]], 0)
     iota(R("ones"), [[0, 516]], 1)
+    iota(R("k16"), [[0, 4], [1, 16]], 0)
+    iota(R("m16"), [[0, 4], [1024, 16]], 0)
     op("g", lambda: g.affine_select(T.et[:], T.ones[:], [[-1, 516]], A.is_equal, 0.0, 3, 4), [R("ones")], [R("et")])
 
     fill(R("zero"), 0.0)
     fill(R("kin"), 0.0)
-    act(R("kt", 2, 1040, 4), R("zero"))
-    act(R("kt", 3, 1040, 4), R("zero"))
-    act(R("kt", 512, 1040, 520), R("zero", 0, 2))
-    act(R("st", 2, 512, 4), R("zero", 0, 128))
-    act(R("st", 3, 512, 4), R("zero", 0, 128))
-    for n, w in (("p4", 4), ("p6", 6)):
-        for k in range(w):
-            c = -8.0 if k == 0 else 0.0 if k == w - 1 else -4096.0
-            act(R(n, k, None, w), R("zero", 0, 144 if w == 4 else 72), F.Identity, bias=c)
-    for c, sh in enumerate([3, 2, 1, 0, 4]):
+    act(R("kt", 65, 1088, 2), R("zero"), F.Copy)
+    act(R("kt", 0, 64), R("zero", 0, 64), F.Copy)
+    act(R("st", 1, 512, 2), R("zero", 0, 256), F.Copy)
+    for c, sh in enumerate([4, 3, 2, 1, 0]):
         ts(col("ib", c), col("pi", 0), sh, 1, A.logical_shift_right, A.bitwise_and)
-    ts(col("ib", 5), col("pi", 0), 3, None, A.bitwise_and)
-    ts(col("ib", 6), col("pi", 0), 2, 3, A.logical_shift_right, A.bitwise_and)
-    ts(col("ib", 7), col("pi", 0), 15, None, A.bitwise_and)
-    ts(R("fb", 12, 16), R("ib", 0, 4), 2.0, -1.0, A.mult, A.add)
+    ts(col("fb", 5), col("ib", 0), -1.0, 1.0, A.mult, A.add)
     cp(R("fb", 0, 5), R("ib", 0, 5))
-    ts(col("fb", 16), col("ib", 4), -1.0, 1.0, A.mult, A.add)
-    ts(col("ib", 8), col("pi", 0), 7, None, A.bitwise_and)
-    for k, c in ((0, -8192.0), (2, 0.0)):
-        ts(R("lv", k, 576, 4), R("zero", 0, 144), c, None, A.add)
-    ts(R3("ksrc", 1, s(0, 4)), R("fb", 12, 16), col("fb", 4), None, A.mult)
-    ts(R3("ksrc", 0, s(0, 4)), R("fb", 12, 16), col("fb", 16), None, A.mult)
-    op("v", lambda: V.tensor_reduce(T.fb[:, 17:18], T.fb[:, 0:4], AxisListType.X, A.add), [R("fb", 0, 4)], [col("fb", 17)])
-    ts(col("fb", 18), col("fb", 16), -10.0, 1.0, A.mult, A.add)
+    fill(R("tab0"), float(EMPTY))
+    ts(R3("ksrc", 0, ALL), R("ib", 1, 5), 0.5, col("fb", 5), A.subtract, A.mult)
+    ts(R3("ksrc", 1, ALL), R("ib", 1, 5), 0.5, col("fb", 0), A.subtract, A.mult)
+    ts(R("lv", 0, 512, 2), R("s4", 0, 512, 2), U, -2.0, A.mult, A.add)
     for a in range(4):
-        cp(N("kin", s(32 * a, 32 * a + 32), s(0, 2), s(16 + 32 * a, 20 + 32 * a)), N("ksrc", s(32 * a, 32 * a + 32), s(0, 2), s(0, 4)))
-    cp(R("fb", 5, 9), R("ib", 5, 9))
-    tt(col("fb", 19), col("fb", 18), col("fb", 17), A.subtract)
-    for y in range(2):
-        for var in range(2):
-            tr(R("kt", 520 * y + var, 520 * y + 512, 4), R3("kin", var, s(16 - 16 * y, 144 - 16 * y)))
-    quant("k", 0, R("kt", 0, 512))
+        cp(N("kin", s(32 * a, 32 * a + 32), ALL, s(16 + 32 * a, 20 + 32 * a)), N("ksrc", s(32 * a, 32 * a + 32), ALL, ALL))
     quant("u", 0, R("us"))
+    act(col("fb", 9), col("fb", 5), bias=-U, scale=-10.0 * U)
+    act(R("junk", 0, 8), R("ksrc"), acc=col("fb", 6))
+    act(col("fb", 10), col("fb", 3), bias=col("fb", 4), scale=2.0)
+    act(col("fb", 11), col("fb", 1), bias=col("fb", 2), scale=2.0)
+    act(R("p4"), R("s4"), F.Relu, bias=-16.0 * U, scale=8.0 * U * U)
+    act(col("fb", 7), col("fb", 6), bias=1.0, scale=0.5)
+    act(col("fb", 8), col("fb", 6), bias=col("fb", 9), scale=-U)
+    act(col("fb", 16), col("fb", 6), bias=-1.0, scale=-1.0)
+    act(col("fb", 14), col("fb", 11), bias=col("fb", 10), scale=4.0)
+    act(R("fb", 20, 24), R("s4", 0, 4), F.Abs, bias=col("fb", 11), scale=-U)
+    act(R("p6"), R("s6"), F.Relu, bias=-96.0 * U, scale=24.0 * U * U)
 
-    def constants_1():
-        cp(R3("ab", s(0, 4), s(129, 145)), R("zero", 0, 64))
-        cp(R3("ab", s(0, 4), s(0, 1)), R("zero", 0, 4))
-        cp(R("wk", 31, 576, 32), R("zero", 0, 18))
-        for k, c in ((1, -8192.0), (5, 0.0), (13, 0.0), (17, 0.0)):
-            ts(R("o3", k, 1728, 24), R("zero", 0, 72), c, None, A.add)
-
-    def ramps():
-        tt(R3("dd", s(0, 2), s(0, 32)), R3("cd", s(0, 2), s(0, 32)), R3("cd", s(0, 2), s(1, 33)), A.subtract)
+    def lists():
+        act(col("fb", 12), col("fb", 14), bias=8.0)
+        act(R("fb", 24, 28), R("fb", 20, 24), F.Relu, bias=1.0, scale=-1.0)
+        act(R3("dd", ALL, s(0, 32)), R3("dd", ALL, s(32, 64)), F.Copy, scale=U)
+        act(R("lrow"), R("lrow"), bias=col("fb", 14))
+        act(R("fb", 28, 32), R("fb", 24, 28), F.Copy, scale=256.0)
         for n in (32, 64, 128, 256):
-            act(R3("dd", s(0, 2), s(n, 2 * n)), R3("dd", s(0, 2), s(0, n)))
-
-    def masks():
-        ts(R("fb", 20, 24), R("i4"), col("fb", 6), None, A.is_equal)
-        act(R("val"), R("val0"), F.Identity, bias=col("fb", 5))
-        act(R("kc"), R("kc0"), F.Identity, bias=col("fb", 7))
-        act(R("own1"), R("own0"), F.Identity, bias=col("fb", 5))
+            act(R3("dd", ALL, s(n, 2 * n)), R3("dd", ALL, s(0, n)), F.Copy)
+            if n == 32:
+                act(col("lrow", 4), col("fb", 1), bias=col("fb", 12), scale=216.0)
+        act(R("xw0", 1024, 2048), X(0), F.Copy)
         for k in range(4):
-            act(R("own", k, 256, 4), R("own1", k, 256, 4), F.Identity, bias=-4096.0, scale=col("fb", 20 + k))
+            act(R("own", k, 256, 4), R("row", k, 256, 4), bias=col("fb", 28 + k), scale=col("fb", 24 + k))
 
-    small = [
-        ramps,
-        masks,
-        lambda: ts(col("fb", 9), col("fb", 8), 0.0, None, A.is_equal),
-        lambda: ts(R("lt"), R("i4", 0, 2), 0.0, col("fb", 8), A.mult, A.add),
-        lambda: ts(R("fb", 10, 12), R("i4", 0, 4, 2), col("fb", 0), 8.0, A.add, A.add),
-        lambda: ts(col("ib", 9), col("pi", 0), 1, 7, A.logical_shift_right, A.bitwise_and),
-        lambda: ts(R("lj"), R("fb", 10, 12), col("fb", 9), col("fb", 8), A.mult, A.add),
-        lambda: ts(col("fb", 25), col("fb", 3), 2.0, col("fb", 5), A.mult, A.subtract),
-        lambda: cp(col("fb", 24), col("ib", 9)),
-        lambda: ts(R("mk"), R("k8"), col("fb", 24), None, A.is_equal),
-    ]
+    LEVEL = {4: (("lv", 1, 512, 2), 1.0, ("pen", 0, 256), ("wk", 0, 512, 2)),
+             3: (("o3", 9, 1536, 12), 1.0 + 8 * U, ("pen", 256, 384), ("wk", 1, 512, 4)),
+             2: (("o2", 5, 384, 6), 1.0 + 24 * U, ("pen", 384, 448), ("wk", 3, 512, 8))}
+    FULL = 1.0 + 56 * U
 
-    def gap():
-        if small:
-            small.pop(0)()
+    def pen(v):
+        src, lim, p, _o = LEVEL[v]
+        ts(R(*p), R(*src), lim, -1.0, A.is_gt, A.mult)
 
-    def pen(a, c, src, lim):
-        ts(R("pen", a, 512, c), src, lim, -BIG, A.is_gt, A.mult)
+    def knock(v):
+        src, _l, p, out = LEVEL[v]
+        scan(R(*out), R(*p), R(*src), 0.0, A.min, A.add)
 
-    def knock(a, c, src):
-        scan(R("wk", a, 512, c), R("pen", a, 512, c), src, 0.0, A.min, A.add)
+    def skip(k, a, w, up, down):
+        ts(R3("dd", k, s(a, 512, w)), R("wk", a, 512, w), FULL, up * U, A.is_gt, A.add)
+        ts(R3("dd", k, s(a + 1, 512, w)), R("wk", a, 512, w), FULL, down * U - 1.0, A.is_le, A.add)
 
     for t in range(ROUNDS):
-        xn, xo, xw, tab, ln = "x%d" % (t + 1), "x%d" % t, "xw%d" % t, "tab%d" % t, "l%d" % t
+        xw, yw, tab, oe, le, yn, ln = ["%s%d" % (n, t) for n in ("xw", "yw", "tab", "oe", "le", "y", "l")]
         for h in range(2):
-            quant("x", 128 * h, R(xo, 512 * h, 512 * h + 512))
+            quant("x", 128 * h, X(t, 512 * h, 512 * h + 512))
             mm(h, "u", 0, "x", 128 * h)
         if t == 0:
-            quant("k", 128, R("kt", 520, 1032))
-            quant("k", 256, R("kt", 1, 513))
+            for y in range(2):
+                for var in range(2):
+                    tr(R("kt", 64 + 512 * y + 2 * var, 576 + 512 * y, 4), R3("kin", var, s(16 - 16 * y, 144 - 16 * y)))
+        else:
+            op("s", lambda: g.sync.dma_start(T[xw][:, 0:1024], X(t)[0]), [X(t)], [R(xw, 0, 1024)], sem="win1", inc=16)
         for h in range(2):
-            ts(R("st", h, 512, 4), PS(h), 0.0, None, A.is_ge)
+            ts(R("st", 2 * h, 512, 4), PS(h), 0.0, None, A.is_ge)
         if t == 0:
-            quant("k", 384, R("kt", 521, 1033))
+            quant("k", 0, R("kt"), 272)
         quant("s", 0, R("st"))
+        for bank, a in ((2, 16), (3, 144), (6, 144), (4, 0), (5, 128)):
+            mm(bank, "k", a, "s", 0)
+        act(R3("ab0", 1, s(1, 128)), PS(6, 127), F.Relu, bias=col("fb", 16), scale=2.0)
+        for y in range(2):
+            act(R("junk", 128 * y, 128 * y + 128), PS(4 + y), F.Relu, bias=col("fb", 8), scale=2.0 * U, acc=col("car", y))
         if t == 0:
-            constants_1()
+            ts(R("o3", 1, 1536, 4), R("s6"), 0.0, -2.0, A.is_equal, A.mult)
+            tt(R3("dd", ALL, s(32, 64)), R3("cd", ALL, s(0, 32)), R3("cd", ALL, s(1, 33)), A.subtract)
+            lists()
+        else:
+            act(R(xw, 1024, 2048), X(t), F.Copy)
+        ts(R3("ab1", 0, ALL), PS(2), col("fb", 7), 1.0 + U, A.is_equal, A.mult)
+        ts(R3("ab0", 0, s(1, 128)), PS(2, 127), col("fb", 7), None, A.is_equal)
+        ts(R3("ab1", 1, ALL), PS(3), col("fb", 7), 1.0 + U, A.is_equal, A.mult)
         for y in range(2):
-            mm(2 + y, "k", 128 * y, "s", 0)
-            mm(4 + y, "k", 256 + 128 * y, "s", 0)
-            act(R("junk", 128 * y, 128 * y + 128), PS(4 + y), F.Relu, bias=col("fb", 19), acc=col("car", y))
-        if t > 0:
-            act(R(xw, 0, 1024), R(xo))
-            act(R(xw, 1024, 2048), R(xo))
+            scan(R3("cs", y, ALL), R3("ab1", y, ALL), R3("ab0", y, ALL), -8.0 * U, A.add, A.subtract)
         for y in range(2):
-            ts(R3("ab", y, s(1, 129)), PS(2 + y), col("fb", 17), -BIG, A.is_equal, A.mult)
-            ts(R3("ab", 2 + y, s(1, 129)), PS(2 + y), col("fb", 17), BIG + 1.0, A.is_equal, A.mult)
-        for y in range(2):
-            scan(R3("cs", y, s(0, 144)), R3("ab", y, s(0, 144)), R3("ab", 2 + y, s(1, 145)), col("car", y), A.add, A.add)
-        for y in range(2):
-            ts(R3("d4", s(0, 9), y, s(0, 16)), R3("cs", y, s(0, 144)), -8.0, 0.0, A.add, A.max)
-        gap()
-        tr(R("lv", 1, 576, 2), R("d4"))
-        gap()
-        if t == 0:
-            act(R(xw, 1024, 2048), R(xo))
-        scan(R("o3", 0, 1728, 3), R("lv"), R("p4"), 0.0, A.add, A.max)
-        pen(0, 2, R("lv", 1, 512, 2), BIG)
-        gap()
-        gap()
-        scan(R("o2"), R("o3", 1, 1728, 4), R("p6"), 0.0, A.add, A.max)
-        knock(0, 2, R("lv", 1, 512, 2))
-        pen(1, 4, R("o3", 9, 1536, 12), BIG)
-        tt(R("c2", 0, 3), R("o3", 1641, 1700, 24), R("o3", 1653, 1710, 24), A.add)
-        tt(R("in1"), R("o2", 5, 432, 12), R("o2", 11, 432, 12), A.add)
-        pen(3, 8, R("o2", 5, 384, 6), BIG)
-        ts(R("dl", 5, 8), R("c2", 0, 3), 8.0, None, A.min)
-        knock(1, 4, R("o3", 9, 1536, 12))
-        gap()
-        ts(R("o1"), R("in1"), -8.0, 0.0, A.add, A.max)
-        pen(7, 16, R("in1", 0, 32), BIG + 8.0)
-        knock(3, 8, R("o2", 5, 384, 6))
-        ts(R("dl", 3, 5), R("in1", 34, 36), 8.0, None, A.min)
-        gap()
-        tt(R("wk", 15, 576, 32), R("o1", 0, 36, 2), R("o1", 1, 36, 2), A.add)
-        knock(7, 16, R("o1", 0, 32))
-        gap()
-        gap()
-        scan(R("sp"), R3("dd", 0, s(0, 512)), R("wk", 0, 512), 0.0, A.add, A.max)
-        scan(R("sm"), R3("dd", 1, s(0, 512)), R("wk", 0, 512), 0.0, A.add, A.max)
-        ts(R("opos"), R("sp", 31, 512, 32), 7.0 - BIG, None, A.add)
-        ts(col("dl", 1), col("wk", 559), -8.0, None, A.add)
+            ts(R3("d4", ALL, y, ALL), R3("cs", y, ALL), col("car", y), 0.0, A.add, A.max)
         for h in range(2):
-            ts(R("omp", 8 * h, 8 * h + 8), R("sm", 31 + 32 * h, 512, 64), 7.0 - BIG, None, A.add)
+            tr(R("lv", 1 + 256 * h, 256 + 256 * h, 2), R3("d4", s(4 * h, 4 * h + 4), ALL, ALL))
+        for h in range(2):
+            scan(R("o3", 768 * h, 768 * h + 768, 3), R("lv", 256 * h, 256 * h + 256), R("p4", 0, 256), 0.0, A.add, A.max)
+        pen(4)
+        for h in range(2):
+            scan(R("o2", 192 * h, 192 * h + 192), R("o3", 768 * h + 1, 768 * h + 768, 4), R("p6", 0, 192), 0.0, A.add, A.max)
+        pen(3)
+        knock(4)
+        tt(R("wk", 7, 512, 16), R("o2", 5, 384, 12), R("o2", 11, 384, 12), A.add)
+        pen(2)
+        knock(3)
+        if t == 0:
+            cp(R("lo"), R("lrow"))
+        skip(0, 7, 16, 248, -256)
+        tt(R("wk", 15, 512, 32), R("wk", 7, 512, 32), R("wk", 23, 512, 32), A.add)
+        tt(R("wk", 31, 512, 32), R("wk", 7, 512, 32), R("wk", 23, 512, 32), A.max)
+        knock(2)
+        skip(1, 7, 32, 392, -400)
+        skip(1, 23, 32, 424, -432)
+        scan(R("sp"), R3("dd", 0, ALL), R("wk"), 0.0, A.add, A.max)
+        scan(R("sm"), R3("dd", 1, ALL), R("wk"), 0.0, A.add, A.max)
+        ts(R("opos"), R("sp", 31, 512, 32), 1024.0, -1073.0, A.mult, A.add)
         scatter(R(tab), R("opos"), R("val"))
-        scan(R("th"), R("dl"), R("dl"), 0.0, A.add, A.max)
-        tt(R("dj", 1, 8), R("da", 1, 8), R("dl", 1, 8), A.subtract)
-        gap()
+        for h in range(2):
+            ts(R("omp", 8 * h, 8 * h + 8), R("sm", 31 + 32 * h, 512, 64), 1024.0, -1625.0, A.mult, A.add)
+        act(R("sg"), R(tab), F.Sign, bias=300.0, scale=-1.0, off=R("lo"))
+        act(R("lin"), R(tab), F.Copy, off=R("lo"))
         for h in range(2):
             tt(R("mm", 128 * h, 128 * h + 128), R(tab), R("own", 128 * h, 128 * h + 128), A.min, off=R("omp", 8 * h, 8 * h + 8))
-        scan(R("mx4", 0, 128), R("s4", 0, 128), R("mm", 0, 128), 0.0, A.add, A.max)
-        tt(R("cmp"), R("th"), R("kc"), A.is_le, off=R("lt"))
-        gap()
-        scan(R("mx4", 128, 256), R("s4", 0, 128), R("mm", 128, 256), 0.0, A.add, A.max)
-        ts(R("oz", 0, 32), R("mx4", 3, 128, 4), 1024.0, None, A.add)
-        tt(R("prod"), R("dj"), R("cmp"), A.mult, off=R("lj"))
-        ts(R("oz", 32, 64), R("mx4", 131, 256, 4), 1024.0, None, A.add)
+        scan(R("mx4", 0, 128), R("s4", 0, 128), R("mm", 0, 128), 0.0, A.min, A.max)
+        scan(R("cum"), R("sg"), R("ones", 0, 128), 32.0, A.add, A.add)
+        scan(R("mx4", 128, 256), R("s4", 0, 128), R("mm", 128, 256), 0.0, A.min, A.max)
+        for c in range(4):
+            act(R("junk", 128 * c, 128 * c + 128), R("cum"), F.Sign, bias=col("lrow", c), scale=-0.4999, acc=col("acc", c))
+        act(R("mp"), R("own"), F.Copy)
+        ts(R("oz", 0, 32), R("mx4", 3, 128, 4), 4.0, col("fb", 10), A.mult, A.add)
+        if t == 0:
+            act(R("sel"), R("own"), F.Sign)
+            ts(R("mk"), R("k16"), col("fb", 14), None, A.is_equal)
+        ts(R("oz", 32, 64), R("mx4", 131, 256, 4), 4.0, col("fb", 10), A.mult, A.add)
 
         def meet(a, b):
-            tt(R("zt", 16 * a, 16 * b), R(xw), R(xo, 16 * a, 16 * b), A.add, off=R("oz", a, b))
+            tt(R("zt", 16 * a, 16 * b), R(xw), X(t, 16 * a, 16 * b), A.add, off=R("oz", a, b))
 
         def layer(h):
             quant("z", 128 * h, R("zt", 512 * h, 512 * h + 512))
             for b in range(4):
                 mm(4 * h + b, "w", 128 * b, "z", 128 * h)
 
+        def half(h):
+            a, b = 128 * h, 128 * h + 128
+            quant(yn, a, R(yw, 1024 + 4 * a, 1024 + 4 * b))
+            send(("one%d", "two%d")[h] % t, [[(R(n + yn, a, b), R(n + ln, a, b), eng)] for n in "qs"])
+
         meet(0, 32)
-        scan(R("s8"), R("m8", 0, 32), R("prod"), 0.0, A.mult, A.add)
-        meet(32, 40)
+        meet(32, 42)
         layer(0)
         for b in range(4):
-            act(R(xn, b, 512, 4), PS(b), scale=0.015625)
-        ts(R("oi"), R("s8", 7, 32, 8), col("fb", 7), None, A.add)
-        meet(40, 64)
-        tt(R("me"), R(tab), R("mk"), A.mult, off=R("oi"))
+            out_of_psum("a", R(yw, 1024 + b, 1536, 4), b, 0.015625)
+        ts(R("oi"), R("acc"), 0.5, 64.0, A.mult, A.add)
+        meet(42, 64)
+        tt(R("me"), R("lin"), R("mk"), A.mult, off=R("oi"))
         layer(1)
-        scan(R("me8"), R("m8"), R("me"), 0.0, A.mult, A.add)
-        if t == 0:
-            quant(ln, 128, R("zero2"))
-        for k in range(2):
-            ts(R("oe", 8 * k, 8 * k + 8), R("me8", 7, 64, 8), col("fb", 25), 1024.0 + k, A.add, A.add)
+        scan(R("me16"), R("m16"), R("me"), 0.0, A.min, A.add)
+        cp(R(oe), R("me16", 15, 64, 16))
+        send("lst%d" % t, [[(R(oe), R(le, 0, 4), eng)]])
+        half(0)
         for b in range(4):
-            if b % 2 == 0:
-                act(R(xn, 512 + b, 1024, 4), PS(4 + b), scale=0.015625)
-            else:
-                ts(R(xn, 512 + b, 1024, 4), PS(4 + b), 0.015625, None, A.mult)
-        act(R("bt", 1, 256, 2), R(xn), off=R("oe", 8, 16))
-        cp(R("bt", 0, 256, 2), R(xn), off=R("oe", 0, 8))
-        quant(ln, 0, R("bt"))
-        srcs = [R("q" + ln, 0, 64), R("s" + ln, 0, 256)]
-        dsts = [R("q" + ln, 256, 320), R("s" + ln, 256, 512)]
-        order("g", srcs, [])
-        per = len(eng) // 2
-        g.remote_dma_fused([RemoteDMATransfer(dst_ids=[DstId(rid=rid, pnc=pid)], dma_engine_mask=sum(1 << e for e in eng[per * k:per * k + per]),
-                                              remote_sem=T.sem["arr%d" % t], src=u8(srcs[k]), dst=u8(dsts[k])) for k in range(2)],
-                           local_sem=T.sem["sent%d" % t])
-        count["sent%d" % t] = count["arr%d" % t] = 2 * per
-        note(("arr%d" % t, 2 * per, {}), [], dsts)
+            out_of_psum("av"[b % 2], R(yw, 1536 + b, 2048, 4), 4 + b, 0.015625)
+        act(R("mr"), R("sel"), F.Copy, off=R(oe))
+        half(1)
         if t == 0:
-            iota(R("tab1"), [[0, 512]], 4096)
-            iota(R("tab2"), [[0, 512]], 4096)
-            for b in (0, 2, 1, 3):
+            iota(R("tab1"), [[0, 528]], EMPTY)
+            iota(R("tab2"), [[0, 528]], EMPTY)
+            for b in range(4):
                 quant("e", 128 * b, R("et", 3 - b, 515 - b))
         if t == 1:
+            load("s", R("vs"), T.v[:], "ldv")
             iota(R("att", 0, 16), [[0, 16]], 0)
-            iota(R("att", 16, 256), [[0, 240]], -1)
-            iota(R("att", 256, 512), [[1, 32], [0, 8]], 0)
+            iota(R("att", 16, 232), [[0, 216]], -1)
+            iota(R("att", 232, 296), [[0, 64]], 1)
+            iota(R("att", 296, 528), [[1, 29], [0, 8]], 2)
+        tt(R("new"), R("row"), R("mr"), A.mult, off=R(le, 0, 4))
+        if t == ROUNDS - 1:
             quant("v", 0, R("vs"))
-        if t < ROUNDS - 1:
-            quant("l%d" % (t + 1), 128, R("zero2"))
-        else:
+        scatter(R("mp"), R(oe), R("new"))
+        if t == ROUNDS - 1:
             for h in range(2):
-                ts(R("onat", 8 * h, 8 * h + 8), R("sp", 31 + 32 * h, 512, 64), 7.0 - BIG, None, A.add)
-            act(R("atr"), R("att"), off=R("onat"))
-            store("s", T.ob[:], N("atr", s(0, 128, 16), s(0, 256)))
-        for b in (0, 2, 1, 3):
-            mm(b, "e", 128 * b, ln, 192)
-            cp(R("came", 128 * (b % 2) + b // 2, 128 * (b % 2) + 128, 2), PS(b, 64))
-        scatter(R(xn), R("oe"), R("came"))
+                ts(R("onat", 8 * h, 8 * h + 8), R("sp", 31 + 32 * h, 512, 64), 1024.0, -1073.0, A.mult, A.add)
+        scan(R("mx2"), R("s4", 0, 256), R("mp"), 0.0, A.min, A.max)
+        ts(R("ox"), R("mx2", 3, 256, 4), 4.0, col("fb", 10), A.mult, A.add)
+        for h in range(2):
+            for b in range(4):
+                mm(4 * h + b, "e", 128 * b, ln, 128 * h)
+                out_of_psum("av"[h * (b % 2)], R(yw, 512 * h + b, 512 * h + 512, 4), 4 * h + b, 1.0)
+            if t == ROUNDS - 1 and h == 0:
+                act(R("atr"), R("att"), F.Copy, off=R("onat"))
+                store("s", T.ob[:], N("atr", s(0, 128, 16), s(0, 256)))
+        for h in range(2):
+            cp(X(t + 1, 512 * h, 512 * h + 256), R(yw), off=R("ox", 32 * h, 32 * h + 16))
+            act(X(t + 1, 512 * h + 256, 512 * h + 512), R(yw), F.Copy, off=R("ox", 32 * h + 16, 32 * h + 32))
 
     for h in range(2):
-        quant("x", 128 * h, R("x%d" % ROUNDS, 512 * h, 512 * h + 512))
+        quant("x", 128 * h, X(ROUNDS, 512 * h, 512 * h + 512))
         mm(h, "v", 0, "x", 128 * h)
-    store("s", T.oc[:], R("qx"))
+        store("s", T.oc[:, 512 * h:512 * h + 512], R("qx", 128 * h, 128 * h + 128))
     for k in range(4):
         store("a", T.osc[4 * k:4 * k + 4, :], N("sx", s(32 * k, 32 * k + 4), s(0, 256)))
     for h in range(2):
         cp(R("ys", 128 * h, 128 * h + 128), PS(h))
-    store("s", T.y[:], R("ys"))
+        store("s", T.y[:, 128 * h:128 * h + 128], R("ys", 128 * h, 128 * h + 128))
     for sem, val in count.items():
-        wait("g" if sem in ("g", "sent0", "sent1", "sent2") else "s", (sem, val, {}))
+        wait("g" if sem in ("g", "sent") else "s", (sem, val, {}))

import numpy as np
from concourse.bass import DstId, RemoteDMATransfer
from concourse.mybir import dt, AluOpType, ActivationFunctionType

A = AluOpType
F = ActivationFunctionType
ROUNDS = 3
U = 2.0 ** -10
EMPTY = 512
SCRATCH = {}
for _d, _l in {
    "bfloat16": dict(us=512, vs=512, kt=1088, kin=[2, 144], et=516, ones=516, zero=512, st=512, zt=1024, junk=512,
                     ab0=[2, 128], s4=512, s6=384, p4=512, p6=384, dd=[2, 512], pen=448, val=256, row=256, tab0=528, tab1=528, tab2=528,
                     sg=128, cum=128, lin=128, mk=64, k16=64, m16=64, me=64, me16=64, att=528, sel=256, mr=64,
                     xw0=2048, xw1=2048, xw2=2048, yw0=2048, yw1=2048, yw2=2048, x0=1024, x1=1024, x2=1024, x3=1024),
    "float8_e4m3fn_x4": dict(qu=128, qv=128, qw=512, qx=256, qz=256, qs=128, qk=272, qe=512, qy0=256, qy1=256, qy2=256, ql0=256, ql1=256, ql2=256),
    "uint8": dict(su=128, sv=128, sw=512, sx=256, sz=256, ss=128, sk=272, se=512, sy0=256, sy1=256, sy2=256, sl0=256, sl1=256, sl2=256),
    "float16": dict(ab1=[2, 128], cs=[2, 128], d4=256, lv=512, o3=1536, o2=384, wk=512, sp=512, sm=512, mm=256, mx4=256, mx2=256),
    "float32": dict(ksrc=[2, 4], fb=32, car=2, acc=4, lrow=8, cd=[2, 33], own=256, mp=256, new=64, atr=256, ys=256),
    "int32": dict(pi=2, ib=6),
    "uint16": dict(opos=16, omp=16, onat=16, oz=64, ox=64, oi=4, oe0=4, oe1=4, oe2=4, le0=8, le1=8, le2=8, lo=8),
}.items():
    for _n, _s in _l.items():
        SCRATCH[_n] = ("sbuf", [128] + (_s if isinstance(_s, list) else [_s]), _d)
SCRATCH["d4"] = ("sbuf", [128, 8, 2, 16], "float16")
for _t in range(8):
    SCRATCH["ps%d" % _t] = ("psum", [128, 512], "float32")

SEMAPHORES = ["v", "a", "p", "g", "ldx", "ldy", "ldu", "ldw", "lds", "ldv", "win0", "win1", "sent", "out"] + [
    "%s%d" % (_n, _t) for _n in ("lst", "one", "two") for _t in range(ROUNDS)]


def rank_program(g, core, T, topo):
    rank = T.rank_of(core)
    if rank is None:
        return
    nxt = T.cores[(rank + 1) % len(T.cores)]
    rid, pid, _ = topo.addr(nxt)
    eng = topo.engines(core, nxt)

    Q = {"v": g.vector, "a": g.scalar, "p": g.tensor, "g": g, "s": g.sync}
    V = g.vector
    count = {}
    known = {e: {} for e in Q}
    log = {}
    s = slice
    ALL = s(None)

    def N(name, *idx):
        where, shape, _d = SCRATCH[name]
        m = np.zeros(shape, bool)
        m[s(None) if where == "psum" else idx] = True
        return (T[name][idx if len(idx) > 1 else idx[0]], name, m, where == "psum")

    def R(name, a=None, b=None, c=None):
        return N(name, s(None)) if a is None else N(name, s(None), s(a, b, c))

    def R3(name, *idx):
        return N(name, s(None), *idx)

    def col(name, c):
        return R(name, c, c + 1)

    def wait(e, tok):
        sem, val, clock = tok
        if known[e].get(sem, 0) >= val:
            return
        Q[e].wait_ge(T.sem[sem], val)
        known[e][sem] = val
        for k2, v2 in clock.items():
            known[e][k2] = max(known[e].get(k2, 0), v2)

    def order(e, reads, writes):
        deps = {}
        for r, wr in [(x, False) for x in reads] + [(x, True) for x in writes]:
            for m, tok, w2 in log.get(r[1], []):
                if (wr or w2 or (r[3] and tok[0] != e)) and known[e].get(tok[0], 0) < tok[1] and deps.get(tok[0], (0, 0))[1] < tok[1] and (m & r[2]).any():
                    deps[tok[0]] = tok
        for tok in sorted(deps.values(), key=lambda t: -len(t[2])):
            wait(e, tok)

    def note(tok, reads, writes):
        for r in reads:
            log.setdefault(r[1], []).append((r[2], tok, False))
        for r in writes:
            log.setdefault(r[1], []).append((r[2], tok, True))

    def op(e, make, reads, writes, sem=None, inc=1):
        reads = [x for x in reads if isinstance(x, tuple)]
        order(e, reads, writes)
        sem = sem or e
        make().then_inc(T.sem[sem], inc)
        count[sem] = count.get(sem, 0) + inc
        tok = (sem, count[sem], dict(known[e]))
        note(tok, reads, writes)
        return tok

    def ap(x, off=None):
        if off:
            return x[0].indirect(off[0])
        return x[0] if isinstance(x, tuple) else x

    def ts(out, in0, s1, s2, *o):
        op("v", lambda: V.tensor_scalar(out[0], in0[0], ap(s1), ap(s2), *o), [in0, s1, s2], [out])

    def tt(out, in0, in1, o, off=None):
        op("v", lambda: V.tensor_tensor(out[0], ap(in0, off), in1[0], o), [in0, in1, off], [out])

    def cp(out, in_, off=None):
        op("v", lambda: V.tensor_copy(out[0], ap(in_, off)), [in_, off], [out])

    def scatter(win, off, in_):
        op("v", lambda: V.tensor_copy(ap(win, off), in_[0]), [in_, off], [win])

    def scan(out, d0, d1, init, o0, o1):
        op("v", lambda: V.tensor_tensor_scan(out[0], d0[0], d1[0], ap(init), o0, o1), [d0, d1, init], [out])

    def tr(out, in_):
        op("v", lambda: V.transpose(out[0], in_[0]), [in_], [out])

    def fill(out, c):
        op("v", lambda: V.memset(out[0], c), [], [out])

    def quant(n, a, in_, w=128):
        q, sc = R("q" + n, a, a + w), R("s" + n, a, a + w)
        op("v", lambda: V.quantize_mx(q[0], sc[0], in_[0]), [in_], [q, sc])

    def PS(bank, n=128):
        return R("ps%d" % bank, 0, n)

    def mm(bank, w, wa, x, xa):
        o, a, b, c, d = PS(bank), R("q" + w, wa, wa + 128), R("s" + w, wa, wa + 128), R("q" + x, xa, xa + 128), R("s" + x, xa, xa + 128)
        op("p", lambda: g.tensor.matmul_mx(o[0], a[0], b[0], c[0], d[0], True, True), [a, b, c, d], [o])

    def act(out, in_, fn=F.Identity, bias=None, scale=1.0, acc=None, off=None):
        kw = {"scale": ap(scale)}
        if bias is not None:
            kw["bias"] = ap(bias)
        if acc:
            kw["accum_out"] = acc[0]
        op("a", lambda: g.scalar.activation(out[0], ap(in_, off), fn, **kw), [in_, bias, scale, off], [out] + ([acc] if acc else []))

    def out_of_psum(e, dst, bank, scale):
        if e == "a":
            act(dst, PS(bank), F.Copy, scale=scale)
        else:
            ts(dst, PS(bank), scale, None, A.mult)

    def iota(out, pat, base):
        op("g", lambda: g.iota(out[0], pat, base, 0, allow_small_or_imprecise_dtypes=True), [], [out])

    def u8(x):
        return x[0].bitcast(dt.uint8) if x[1][0] == "q" else x[0]

    def load(e, dst, src, sem):
        return op(e, lambda: Q[e].dma_start(u8(dst), src), [], [dst], sem=sem, inc=16)

    def store(e, dst, src):
        order(e, [src], [])
        Q[e].dma_start(dst, u8(src)).then_inc(T.sem.out, 16)
        count["out"] = count.get("out", 0) + 16

    def send(sem, calls):
        for call in calls:
            order("g", [c[0] for c in call], [])
            g.remote_dma_fused([RemoteDMATransfer(dst_ids=[DstId(rid=rid, pnc=pid)], dma_engine_mask=sum(1 << e for e in es),
                                                  remote_sem=T.sem[sem], src=u8(src), dst=u8(dst)) for src, dst, es in call], local_sem=T.sem.sent)
            for k in (sem, "sent"):
                count[k] = count.get(k, 0) + sum(len(c[2]) for c in call)
        note((sem, count[sem], {}), [], [c[1] for call in calls for c in call])

    def X(t, a=0, b=1024, c=None):
        return R("x%d" % t, a, b, c)

    load("a", R("us"), T.u[:], "ldu")
    load("s", X(0, 0, 512), T.x[:, 0:512], "ldx")
    wait("s", load("s", X(0, 512, 1024), T.x[:, 512:1024], "ldy"))
    load("s", R("qw"), T.wc[:], "ldw")
    load("s", R("sw"), T.ws[:], "lds")
    load("s", R("xw0", 0, 1024), T.x[:], "win0")

    op("g", lambda: g.iota(T.pi[:, 0:1], [[0, 1]], 0, 1), [], [col("pi", 0)])
    iota(R3("ab0", ALL, s(0, 1)), [[0, 2]], 0)
    iota(R("s4"), [[0, 128], [1024, 4]], 0)
    iota(R("s6"), [[0, 64], [1024, 6]], 0)
    for k, (pats, bases) in enumerate([([[[8, 16]], [[8, 8]], [[8, 4]], [[64, 2]]], [407, 335, 287, 183]),
                                       ([[[8, 8], [0, 2]], [[8, 4], [0, 2]], [[64, 2], [0, 2]], [[0, 2]]], [343, 303, 215, -41])]):
        for lv in range(4):
            iota(R3("cd", k, s(1 << lv, 33 if lv else 32, 2 << lv)), pats[lv], bases[lv])
    iota(R3("cd", ALL, s(16, 33, 16)), [[-552, 2], [56, 2]], -105)
    iota(R3("cd", ALL, s(0, 1)), [[-64, 2]], -1633)
    iota(R("lrow"), [[264, 2], [16, 4]], 16)
    iota(R("val"), [[16, 8], [128, 2], [1, 16]], 0)
    iota(R("row"), [[1, 256]], 0)
    iota(R("ones"), [[0, 516]], 1)
    iota(R("k16"), [[0, 4], [1, 16]], 0)
    iota(R("m16"), [[0, 4], [1024, 16]], 0)
    op("g", lambda: g.affine_select(T.et[:], T.ones[:], [[-1, 516]], A.is_equal, 0.0, 3, 4), [R("ones")], [R("et")])

    fill(R("zero"), 0.0)
    fill(R("kin"), 0.0)
    act(R("kt", 65, 1088, 2), R("zero"), F.Copy)
    act(R("kt", 0, 64), R("zero", 0, 64), F.Copy)
    act(R("st", 1, 512, 2), R("zero", 0, 256), F.Copy)
    for c, sh in enumerate([4, 3, 2, 1, 0]):
        ts(col("ib", c), col("pi", 0), sh, 1, A.logical_shift_right, A.bitwise_and)
    ts(col("fb", 5), col("ib", 0), -1.0, 1.0, A.mult, A.add)
    cp(R("fb", 0, 5), R("ib", 0, 5))
    fill(R("tab0"), float(EMPTY))
    ts(R3("ksrc", 0, ALL), R("ib", 1, 5), 0.5, col("fb", 5), A.subtract, A.mult)
    ts(R3("ksrc", 1, ALL), R("ib", 1, 5), 0.5, col("fb", 0), A.subtract, A.mult)
    ts(R("lv", 0, 512, 2), R("s4", 0, 512, 2), U, -2.0, A.mult, A.add)
    for a in range(4):
        cp(N("kin", s(32 * a, 32 * a + 32), ALL, s(16 + 32 * a, 20 + 32 * a)), N("ksrc", s(32 * a, 32 * a + 32), ALL, ALL))
    quant("u", 0, R("us"))
    act(col("fb", 9), col("fb", 5), bias=-U, scale=-10.0 * U)
    act(R("junk", 0, 8), R("ksrc"), acc=col("fb", 6))
    act(col("fb", 10), col("fb", 3), bias=col("fb", 4), scale=2.0)
    act(col("fb", 11), col("fb", 1), bias=col("fb", 2), scale=2.0)
    act(R("p4"), R("s4"), F.Relu, bias=-16.0 * U, scale=8.0 * U * U)
    act(col("fb", 7), col("fb", 6), bias=1.0, scale=0.5)
    act(col("fb", 8), col("fb", 6), bias=col("fb", 9), scale=-U)
    act(col("fb", 16), col("fb", 6), bias=-1.0, scale=-1.0)
    act(col("fb", 14), col("fb", 11), bias=col("fb", 10), scale=4.0)
    act(R("fb", 20, 24), R("s4", 0, 4), F.Abs, bias=col("fb", 11), scale=-U)
    act(R("p6"), R("s6"), F.Relu, bias=-96.0 * U, scale=24.0 * U * U)

    def lists():
        act(col("fb", 12), col("fb", 14), bias=8.0)
        act(R("fb", 24, 28), R("fb", 20, 24), F.Relu, bias=1.0, scale=-1.0)
        act(R3("dd", ALL, s(0, 32)), R3("dd", ALL, s(32, 64)), F.Copy, scale=U)
        act(R("lrow"), R("lrow"), bias=col("fb", 14))
        act(R("fb", 28, 32), R("fb", 24, 28), F.Copy, scale=256.0)
        for n in (32, 64, 128, 256):
            act(R3("dd", ALL, s(n, 2 * n)), R3("dd", ALL, s(0, n)), F.Copy)
            if n == 32:
                act(col("lrow", 4), col("fb", 1), bias=col("fb", 12), scale=216.0)
        act(R("xw0", 1024, 2048), X(0), F.Copy)
        for k in range(4):
            act(R("own", k, 256, 4), R("row", k, 256, 4), bias=col("fb", 28 + k), scale=col("fb", 24 + k))

    LEVEL = {4: (("lv", 1, 512, 2), 1.0, ("pen", 0, 256), ("wk", 0, 512, 2)),
             3: (("o3", 9, 1536, 12), 1.0 + 8 * U, ("pen", 256, 384), ("wk", 1, 512, 4)),
             2: (("o2", 5, 384, 6), 1.0 + 24 * U, ("pen", 384, 448), ("wk", 3, 512, 8))}
    FULL = 1.0 + 56 * U

    def pen(v):
        src, lim, p, _o = LEVEL[v]
        ts(R(*p), R(*src), lim, -1.0, A.is_gt, A.mult)

    def knock(v):
        src, _l, p, out = LEVEL[v]
        scan(R(*out), R(*p), R(*src), 0.0, A.min, A.add)

    def skip(k, a, w, up, down):
        ts(R3("dd", k, s(a, 512, w)), R("wk", a, 512, w), FULL, up * U, A.is_gt, A.add)
        ts(R3("dd", k, s(a + 1, 512, w)), R("wk", a, 512, w), FULL, down * U - 1.0, A.is_le, A.add)

    for t in range(ROUNDS):
        xw, yw, tab, oe, le, yn, ln = ["%s%d" % (n, t) for n in ("xw", "yw", "tab", "oe", "le", "y", "l")]
        for h in range(2):
            quant("x", 128 * h, X(t, 512 * h, 512 * h + 512))
            mm(h, "u", 0, "x", 128 * h)
        if t == 0:
            for y in range(2):
                for var in range(2):
                    tr(R("kt", 64 + 512 * y + 2 * var, 576 + 512 * y, 4), R3("kin", var, s(16 - 16 * y, 144 - 16 * y)))
        else:
            op("s", lambda: g.sync.dma_start(T[xw][:, 0:1024], X(t)[0]), [X(t)], [R(xw, 0, 1024)], sem="win1", inc=16)
        for h in range(2):
            ts(R("st", 2 * h, 512, 4), PS(h), 0.0, None, A.is_ge)
        if t == 0:
            quant("k", 0, R("kt"), 272)
        quant("s", 0, R("st"))
        for bank, a in ((2, 16), (3, 144), (6, 144), (4, 0), (5, 128)):
            mm(bank, "k", a, "s", 0)
        act(R3("ab0", 1, s(1, 128)), PS(6, 127), F.Relu, bias=col("fb", 16), scale=2.0)
        for y in range(2):
            act(R("junk", 128 * y, 128 * y + 128), PS(4 + y), F.Relu, bias=col("fb", 8), scale=2.0 * U, acc=col("car", y))
        if t == 0:
            ts(R("o3", 1, 1536, 4), R("s6"), 0.0, -2.0, A.is_equal, A.mult)
            tt(R3("dd", ALL, s(32, 64)), R3("cd", ALL, s(0, 32)), R3("cd", ALL, s(1, 33)), A.subtract)
            lists()
        else:
            act(R(xw, 1024, 2048), X(t), F.Copy)
        ts(R3("ab1", 0, ALL), PS(2), col("fb", 7), 1.0 + U, A.is_equal, A.mult)
        ts(R3("ab0", 0, s(1, 128)), PS(2, 127), col("fb", 7), None, A.is_equal)
        ts(R3("ab1", 1, ALL), PS(3), col("fb", 7), 1.0 + U, A.is_equal, A.mult)
        for y in range(2):
            scan(R3("cs", y, ALL), R3("ab1", y, ALL), R3("ab0", y, ALL), -8.0 * U, A.add, A.subtract)
        for y in range(2):
            ts(R3("d4", ALL, y, ALL), R3("cs", y, ALL), col("car", y), 0.0, A.add, A.max)
        for h in range(2):
            tr(R("lv", 1 + 256 * h, 256 + 256 * h, 2), R3("d4", s(4 * h, 4 * h + 4), ALL, ALL))
        for h in range(2):
            scan(R("o3", 768 * h, 768 * h + 768, 3), R("lv", 256 * h, 256 * h + 256), R("p4", 0, 256), 0.0, A.add, A.max)
        pen(4)
        for h in range(2):
            scan(R("o2", 192 * h, 192 * h + 192), R("o3", 768 * h + 1, 768 * h + 768, 4), R("p6", 0, 192), 0.0, A.add, A.max)
        pen(3)
        knock(4)
        tt(R("wk", 7, 512, 16), R("o2", 5, 384, 12), R("o2", 11, 384, 12), A.add)
        pen(2)
        knock(3)
        if t == 0:
            cp(R("lo"), R("lrow"))
        skip(0, 7, 16, 248, -256)
        tt(R("wk", 15, 512, 32), R("wk", 7, 512, 32), R("wk", 23, 512, 32), A.add)
        tt(R("wk", 31, 512, 32), R("wk", 7, 512, 32), R("wk", 23, 512, 32), A.max)
        knock(2)
        skip(1, 7, 32, 392, -400)
        skip(1, 23, 32, 424, -432)
        scan(R("sp"), R3("dd", 0, ALL), R("wk"), 0.0, A.add, A.max)
        scan(R("sm"), R3("dd", 1, ALL), R("wk"), 0.0, A.add, A.max)
        ts(R("opos"), R("sp", 31, 512, 32), 1024.0, -1073.0, A.mult, A.add)
        scatter(R(tab), R("opos"), R("val"))
        for h in range(2):
            ts(R("omp", 8 * h, 8 * h + 8), R("sm", 31 + 32 * h, 512, 64), 1024.0, -1625.0, A.mult, A.add)
        act(R("sg"), R(tab), F.Sign, bias=300.0, scale=-1.0, off=R("lo"))
        act(R("lin"), R(tab), F.Copy, off=R("lo"))
        for h in range(2):
            tt(R("mm", 128 * h, 128 * h + 128), R(tab), R("own", 128 * h, 128 * h + 128), A.min, off=R("omp", 8 * h, 8 * h + 8))
        scan(R("mx4", 0, 128), R("s4", 0, 128), R("mm", 0, 128), 0.0, A.min, A.max)
        scan(R("cum"), R("sg"), R("ones", 0, 128), 32.0, A.add, A.add)
        scan(R("mx4", 128, 256), R("s4", 0, 128), R("mm", 128, 256), 0.0, A.min, A.max)
        for c in range(4):
            act(R("junk", 128 * c, 128 * c + 128), R("cum"), F.Sign, bias=col("lrow", c), scale=-0.4999, acc=col("acc", c))
        act(R("mp"), R("own"), F.Copy)
        ts(R("oz", 0, 32), R("mx4", 3, 128, 4), 4.0, col("fb", 10), A.mult, A.add)
        if t == 0:
            act(R("sel"), R("own"), F.Sign)
            ts(R("mk"), R("k16"), col("fb", 14), None, A.is_equal)
        ts(R("oz", 32, 64), R("mx4", 131, 256, 4), 4.0, col("fb", 10), A.mult, A.add)

        def meet(a, b):
            tt(R("zt", 16 * a, 16 * b), R(xw), X(t, 16 * a, 16 * b), A.add, off=R("oz", a, b))

        def layer(h):
            quant("z", 128 * h, R("zt", 512 * h, 512 * h + 512))
            for b in range(4):
                mm(4 * h + b, "w", 128 * b, "z", 128 * h)

        def half(h):
            a, b = 128 * h, 128 * h + 128
            quant(yn, a, R(yw, 1024 + 4 * a, 1024 + 4 * b))
            send(("one%d", "two%d")[h] % t, [[(R(n + yn, a, b), R(n + ln, a, b), eng)] for n in "qs"])

        meet(0, 32)
        meet(32, 42)
        layer(0)
        for b in range(4):
            out_of_psum("a", R(yw, 1024 + b, 1536, 4), b, 0.015625)
        ts(R("oi"), R("acc"), 0.5, 64.0, A.mult, A.add)
        meet(42, 64)
        tt(R("me"), R("lin"), R("mk"), A.mult, off=R("oi"))
        layer(1)
        scan(R("me16"), R("m16"), R("me"), 0.0, A.min, A.add)
        cp(R(oe), R("me16", 15, 64, 16))
        send("lst%d" % t, [[(R(oe), R(le, 0, 4), eng)]])
        half(0)
        for b in range(4):
            out_of_psum("av"[b % 2], R(yw, 1536 + b, 2048, 4), 4 + b, 0.015625)
        act(R("mr"), R("sel"), F.Copy, off=R(oe))
        half(1)
        if t == 0:
            iota(R("tab1"), [[0, 528]], EMPTY)
            iota(R("tab2"), [[0, 528]], EMPTY)
            for b in range(4):
                quant("e", 128 * b, R("et", 3 - b, 515 - b))
        if t == 1:
            load("s", R("vs"), T.v[:], "ldv")
            iota(R("att", 0, 16), [[0, 16]], 0)
            iota(R("att", 16, 232), [[0, 216]], -1)
            iota(R("att", 232, 296), [[0, 64]], 1)
            iota(R("att", 296, 528), [[1, 29], [0, 8]], 2)
        tt(R("new"), R("row"), R("mr"), A.mult, off=R(le, 0, 4))
        if t == ROUNDS - 1:
            quant("v", 0, R("vs"))
        scatter(R("mp"), R(oe), R("new"))
        if t == ROUNDS - 1:
            for h in range(2):
                ts(R("onat", 8 * h, 8 * h + 8), R("sp", 31 + 32 * h, 512, 64), 1024.0, -1073.0, A.mult, A.add)
        scan(R("mx2"), R("s4", 0, 256), R("mp"), 0.0, A.min, A.max)
        ts(R("ox"), R("mx2", 3, 256, 4), 4.0, col("fb", 10), A.mult, A.add)
        for h in range(2):
            for b in range(4):
                mm(4 * h + b, "e", 128 * b, ln, 128 * h)
                out_of_psum("av"[h * (b % 2)], R(yw, 512 * h + b, 512 * h + 512, 4), 4 * h + b, 1.0)
            if t == ROUNDS - 1 and h == 0:
                act(R("atr"), R("att"), F.Copy, off=R("onat"))
                store("s", T.ob[:], N("atr", s(0, 128, 16), s(0, 256)))
        for h in range(2):
            cp(X(t + 1, 512 * h, 512 * h + 256), R(yw), off=R("ox", 32 * h, 32 * h + 16))
            act(X(t + 1, 512 * h + 256, 512 * h + 512), R(yw), F.Copy, off=R("ox", 32 * h + 16, 32 * h + 32))

    for h in range(2):
        quant("x", 128 * h, X(ROUNDS, 512 * h, 512 * h + 512))
        mm(h, "v", 0, "x", 128 * h)
        store("s", T.oc[:, 512 * h:512 * h + 512], R("qx", 128 * h, 128 * h + 128))
    for k in range(4):
        store("a", T.osc[4 * k:4 * k + 4, :], N("sx", s(32 * k, 32 * k + 4), s(0, 256)))
    for h in range(2):
        cp(R("ys", 128 * h, 128 * h + 128), PS(h))
        store("s", T.y[:, 128 * h:128 * h + 128], R("ys", 128 * h, 128 * h + 128))
    for sem, val in count.items():
        wait("g" if sem in ("g", "sent") else "s", (sem, val, {}))
